import numpy as np
import ml_dtypes


def mxq(x, axis, fmt="e4m3"):
    dtype, down = {"e4m3": (ml_dtypes.float8_e4m3fn, 7), "e5m2": (ml_dtypes.float8_e5m2, 14)}[fmt]
    v = np.moveaxis(np.asarray(x, np.float32).astype(ml_dtypes.bfloat16).astype(np.float64), axis, -1)
    blocks = v.reshape(v.shape[:-1] + (-1, 32))
    amax = np.abs(blocks).max(-1, keepdims=True)
    byte = np.maximum(np.where(amax > 0, np.frexp(amax)[1] - 1 + 127, 0) - down, 1)
    scale = np.exp2(byte - 127.0)
    codes = (blocks / scale).astype(np.float32).astype(dtype).astype(np.float64)
    return np.moveaxis((codes * scale).reshape(v.shape), -1, axis)


WIDE = False


def mx_kscale(k):
    if not WIDE:
        return np.ones(k)
    levels = np.array([10, -10, 5, -5, 0])
    if k % 512:
        return np.exp2(np.random.permutation(np.resize(levels, k // 32))).repeat(32)
    a = np.empty((k // 512, 16))
    for p in range(k // 512):
        a[p, :8] = np.random.permutation(np.resize(levels, 8))
        for g in range(8):
            far = levels[np.abs(levels - a[p, g]) >= 10]
            a[p, g + 8] = far[np.random.randint(len(far))]
    return np.exp2(a.ravel()).repeat(32)


def f64(x):
    return np.asarray(x).astype(np.float64)


def striped(idx):
    return np.tile(idx.reshape(-1, 16).T, (8, 1)).astype(np.uint16)


def unstriped(offs):
    return offs[:16].T.reshape(-1).astype(np.int64)


def pack_weight(w):
    k, n = w.shape
    w = f64(np.asarray(w, np.float32).astype(ml_dtypes.bfloat16)).reshape(k // 32, 32, n)
    amax = np.abs(w).max(1)
    byte = np.clip(np.where(amax > 0, np.frexp(amax)[1] - 1 + 127 - 7, 1), 1, 254)
    scaled = (w * np.exp2(127.0 - byte)[:, None, :]).reshape(k, n).astype(np.float32)
    words = np.ascontiguousarray(scaled.reshape(k // 512, 128, 4, n).transpose(0, 1, 3, 2)).astype(ml_dtypes.float8_e4m3fn).view(np.uint8)
    return words, np.ascontiguousarray(byte.astype(np.uint8).reshape(k // 512, 16, n))


def unpack_weight(words, scales):
    g, p, n, _ = words.shape
    vals = np.ascontiguousarray(words).view(ml_dtypes.float8_e4m3fn).astype(np.float64) * np.repeat(np.exp2(scales.astype(np.float64) - 127.0), 8, axis=1)[..., None]
    return vals.transpose(0, 1, 3, 2).reshape(g * 512, n)


def silu(v):
    return v / (1.0 + np.exp(-np.maximum(v, -700.0)))


K, T, D, S, V, H, N = 1024, 2048, 2, 768, 384, 512, 128


def setup_inputs():
    n = np.random.standard_normal
    s = mx_kscale(K)[:, None]
    u = mx_kscale(H)
    packed = pack_weight(n((K, T)) * s)
    return {
        "x_words": packed[0],
        "x_scales": packed[1],
        "w1": (n((K, H)) / np.sqrt(K) / s * u).astype(np.float32),
        "w2": (n((H, N)) / np.sqrt(H) / u[:, None]).astype(np.float32),
        "gate": np.tile(np.random.uniform(0.2, 1.0, (D, 1, V)) / np.sqrt(D), (1, N, 1)).astype(np.float32),
        "offs": striped(np.random.permutation(T)[:S]),
        "pos1": striped(np.random.permutation(S)[:V]),
        "pos2": striped(np.random.permutation(S)[:V]),
    }


def reference(x_words, x_scales, w1, w2, gate, offs, pos1, pos2):
    idx = unstriped(offs)
    xq = unpack_weight(x_words, x_scales)[:, idx]
    h = silu(mxq(f64(w1), 0, "e4m3").T @ xq)
    y = mxq(f64(w2), 0, "e4m3").T @ mxq(h, 0, "e4m3")
    return sum(f64(gate[d]) * y[:, unstriped(p)] for d, p in enumerate((pos1, pos2)))

@@ -1,0 +1,158 @@
+from contextlib import ExitStack
+
+import concourse.mybir as mybir
+
+K, T, D, S, V, H, N = 1024, 2048, 2, 768, 384, 512, 128
+FLOPS = 2 * K * H * S + 2 * H * N * S
+
+F32 = mybir.dt.float32
+BF16 = mybir.dt.bfloat16
+I32 = mybir.dt.int32
+U32 = mybir.dt.uint32
+U16 = mybir.dt.uint16
+U8 = mybir.dt.uint8
+FP8X4 = mybir.dt.float8_e4m3fn_x4
+MULT = mybir.AluOpType.mult
+SILU = mybir.ActivationFunctionType.Silu
+
+P = 128
+PACK = 4
+K_PASS = P * PACK
+PASSES = K // K_PASS
+CHUNK = 128
+CHUNKS = S // CHUNK
+GATHER = 256
+STRIPE = 16
+M_SCALAR = (128, 48)
+V_PIECES = 2
+
+
+def tile_picked_sub_mlp_silu_sub_p_kernel(
+    tc, x_words, x_scales, w1, w2, gate, offs, pos1, pos2, out
+):
+    nc = tc.nc
+    with ExitStack() as ctx:
+        keep = ctx.enter_context(tc.tile_pool(name="keep", bufs=1))
+        psum = ctx.enter_context(tc.psum_pool(name="psum", bufs=1))
+        psum_y = ctx.enter_context(tc.psum_pool(name="psum_y", bufs=2))
+
+        offs_sb = keep.tile([P, S // STRIPE], U16, name="offs_sb")
+        pos_sb = [keep.tile([P, V // STRIPE], U16, name=f"pos_sb{d}") for d in range(D)]
+        words_all = [keep.tile([P, T], I32, name=f"words_all{o}", align_bytes=64) for o in range(PASSES)]
+        scales_all = keep.tile([P, T // 4], I32, name="scales_all", align_bytes=64)
+        w1_raw = [keep.tile([P, PACK, H], F32, name=f"w1_raw{o}") for o in range(PASSES)]
+        w2_raw = keep.tile([P, PACK, N], F32, name="w2_raw")
+        gate_sb = keep.tile([P, D, V], F32, name="gate_sb")
+        warm_in = keep.tile([P, 1], F32, name="warm_in")
+        warm_out = keep.tile([P, 1], F32, name="warm_out")
+
+        def load_words(o):
+            nc.sync.dma_start(words_all[o][:], x_words[o].rearrange("p n t -> p (n t)").bitcast(I32))
+
+        def load_w1(o):
+            rows = w1[o * K_PASS : (o + 1) * K_PASS, :]
+            nc.sync.dma_start(w1_raw[o][:], rows.rearrange("(p j) c -> p j c", j=PACK))
+
+        nc.vector.memset(scales_all[:], 0)
+        nc.vector.memset(warm_in[:], 0.0)
+        nc.scalar.activation(warm_out[:], warm_in[:], SILU)
+        nc.sync.dma_start(offs_sb[:], offs)
+        load_w1(0)
+        for q in range(4):
+            nc.sync.dma_start(scales_all[32 * q : 32 * q + 8, :], x_scales[:, 4 * q : 4 * q + 4, :].bitcast(I32))
+        load_words(0)
+        load_w1(1)
+        load_words(1)
+        nc.sync.dma_start(w2_raw[:], w2.rearrange("(p j) m -> p j m", j=PACK))
+        nc.sync.dma_start(gate_sb[:], gate.rearrange("d m v -> m d v"))
+        nc.sync.dma_start(pos_sb[0][:], pos1)
+        nc.sync.dma_start(pos_sb[1][:], pos2)
+
+        x_codes = [keep.tile([P, S], U32, name=f"x_codes{o}", align_bytes=64) for o in range(PASSES)]
+        x_planes = keep.tile([P, S], U8, name="x_planes", align_bytes=64)
+        w1_bf = [keep.tile([P, H * PACK], BF16, name=f"w1_bf{o}", align_bytes=64) for o in range(PASSES)]
+        w1_codes = [keep.tile([P, H], U32, name=f"w1_codes{o}", align_bytes=64) for o in range(PASSES)]
+        w1_scales = [keep.tile([P, H], U8, name=f"w1_scales{o}", align_bytes=64) for o in range(PASSES)]
+        w2_bf = keep.tile([P, N * PACK], BF16, name="w2_bf", align_bytes=64)
+        w2_codes = keep.tile([P, N], U32, name="w2_codes", align_bytes=64)
+        w2_scales = keep.tile([P, N], U8, name="w2_scales", align_bytes=64)
+        pre = [psum.tile([P, PACK, CHUNK], F32, name=f"pre{c}") for c in range(CHUNKS)]
+        h_bf = [keep.tile([P, CHUNK * PACK], BF16, name=f"h_bf{c}", align_bytes=64) for c in range(CHUNKS)]
+        h_codes = [keep.tile([P, CHUNK], U32, name=f"h_codes{c}", align_bytes=64) for c in range(CHUNKS)]
+        h_scales = [keep.tile([P, CHUNK], U8, name=f"h_scales{c}", align_bytes=64) for c in range(CHUNKS)]
+        y_sb = keep.tile([P, S], F32, name="y_sb")
+
+        def gather_words(o, j0, n):
+            entries = offs_sb[:, j0 // STRIPE : (j0 + n) // STRIPE]
+            nc.vector.tensor_copy(x_codes[o][:, j0 : j0 + n], words_all[o][:].bitcast(U32).indirect(entries))
+
+        def quantize_w1(o):
+            src = w1_raw[o][:].rearrange("p j (m t) -> p m j t", t=PACK)
+            dst = w1_bf[o][:].rearrange("p (t m j) -> p m j t", t=PACK, j=PACK)
+            split = M_SCALAR[o]
+            nc.scalar.copy(dst[:, :split], src[:, :split])
+            if split < P:
+                nc.vector.tensor_copy(dst[:, split:], src[:, split:])
+            nc.vector.quantize_mx(w1_codes[o][:].bitcast(FP8X4), w1_scales[o][:], w1_bf[o][:])
+
+        def layer1(o, c):
+            cols = slice(c * CHUNK, (c + 1) * CHUNK)
+            for t in range(PACK):
+                ch = slice(t * P, (t + 1) * P)
+                nc.tensor.matmul_mx(
+                    pre[c][:, t, :],
+                    lhsT=w1_codes[o][:, ch].bitcast(FP8X4),
+                    lhsT_scale=w1_scales[o][:, ch],
+                    rhs=x_codes[o][:, cols].bitcast(FP8X4),
+                    rhs_scale=x_planes[4 * o :, cols],
+                    start=(o == 0 and t == 0),
+                    stop=(o == PASSES - 1 and t == PACK - 1),
+                )
+
+        def layer2(c):
+            nc.vector.quantize_mx(h_codes[c][:].bitcast(FP8X4), h_scales[c][:], h_bf[c][:])
+            y_ps = psum_y.tile([P, CHUNK], F32, name="y_ps")
+            nc.tensor.matmul_mx(
+                y_ps[:],
+                lhsT=w2_codes[:].bitcast(FP8X4),
+                lhsT_scale=w2_scales[:],
+                rhs=h_codes[c][:].bitcast(FP8X4),
+                rhs_scale=h_scales[c][:],
+                start=True,
+                stop=True,
+            )
+            nc.vector.tensor_copy(y_sb[:, c * CHUNK : (c + 1) * CHUNK], y_ps[:])
+
+        nc.vector.tensor_copy(x_planes[:], scales_all[:].bitcast(U8).indirect(offs_sb[:]))
+        quantize_w1(0)
+        for j0 in range(0, S, GATHER):
+            gather_words(0, j0, GATHER)
+        for c in range(CHUNKS):
+            layer1(0, c)
+        quantize_w1(1)
+        for j0 in range(0, S, GATHER):
+            gather_words(1, j0, GATHER)
+        for c in range(CHUNKS):
+            layer1(1, c)
+            nc.scalar.activation(
+                h_bf[c][:].rearrange("p (n t) -> p n t", t=PACK), pre[c][:].rearrange("p t n -> p n t"), SILU
+            )
+        nc.vector.tensor_copy(
+            w2_bf[:].rearrange("p (m j) -> p m j", j=PACK), w2_raw[:].rearrange("p j m -> p m j")
+        )
+        nc.vector.quantize_mx(w2_codes[:].bitcast(FP8X4), w2_scales[:], w2_bf[:])
+        for c in range(CHUNKS):
+            layer2(c)
+
+        width = V // V_PIECES
+        for i in range(V_PIECES):
+            cols = slice(i * width, (i + 1) * width)
+            terms = []
+            for d in range(D):
+                term = keep.tile([P, width], F32, name=f"term{i}_{d}")
+                entries = pos_sb[d][:, cols.start // STRIPE : cols.stop // STRIPE]
+                nc.vector.tensor_tensor(term[:], y_sb[:].indirect(entries), gate_sb[:, d, cols], MULT)
+                terms.append(term)
+            res = keep.tile([P, width], F32, name=f"res{i}")
+            nc.vector.tensor_add(res[:], terms[0][:], terms[1][:])
+            nc.sync.dma_start(out[:, cols], res[:])

@@ -23,7 +23,7 @@ CHUNK = 128
 CHUNKS = S // CHUNK
 GATHER = 256
 STRIPE = 16
-M_SCALAR = (128, 48)
+M_SCALAR = (96, 96)
 V_PIECES = 2
 
 
@@ -54,21 +54,24 @@ def tile_picked_sub_mlp_silu_sub_p_kernel(
             nc.sync.dma_start(w1_raw[o][:], rows.rearrange("(p j) c -> p j c", j=PACK))
 
         nc.vector.memset(scales_all[:], 0)
-        nc.vector.memset(warm_in[:], 0.0)
-        nc.scalar.activation(warm_out[:], warm_in[:], SILU)
         nc.sync.dma_start(offs_sb[:], offs)
         load_w1(0)
+        nc.sync.dma_start(pos_sb[0][:], pos1)
+        nc.sync.dma_start(pos_sb[1][:], pos2)
         for q in range(4):
             nc.sync.dma_start(scales_all[32 * q : 32 * q + 8, :], x_scales[:, 4 * q : 4 * q + 4, :].bitcast(I32))
-        load_words(0)
+        nc.vector.memset(warm_in[:], 0.0)
+        nc.scalar.activation(warm_out[:], warm_in[:], SILU)
         load_w1(1)
+        load_words(0)
         load_words(1)
         nc.sync.dma_start(w2_raw[:], w2.rearrange("(p j) m -> p j m", j=PACK))
         nc.sync.dma_start(gate_sb[:], gate.rearrange("d m v -> m d v"))
-        nc.sync.dma_start(pos_sb[0][:], pos1)
-        nc.sync.dma_start(pos_sb[1][:], pos2)
 
-        x_codes = [keep.tile([P, S], U32, name=f"x_codes{o}", align_bytes=64) for o in range(PASSES)]
+        x_codes = [
+            [keep.tile([P, GATHER], U32, name=f"x_codes{o}_{g}", align_bytes=64) for g in range(S // GATHER)]
+            for o in range(PASSES)
+        ]
         x_planes = keep.tile([P, S], U8, name="x_planes", align_bytes=64)
         w1_bf = [keep.tile([P, H * PACK], BF16, name=f"w1_bf{o}", align_bytes=64) for o in range(PASSES)]
         w1_codes = [keep.tile([P, H], U32, name=f"w1_codes{o}", align_bytes=64) for o in range(PASSES)]
@@ -84,7 +87,7 @@ def tile_picked_sub_mlp_silu_sub_p_kernel(
 
         def gather_words(o, j0, n):
             entries = offs_sb[:, j0 // STRIPE : (j0 + n) // STRIPE]
-            nc.vector.tensor_copy(x_codes[o][:, j0 : j0 + n], words_all[o][:].bitcast(U32).indirect(entries))
+            nc.vector.tensor_copy(x_codes[o][j0 // GATHER][:], words_all[o][:].bitcast(U32).indirect(entries))
 
         def quantize_w1(o):
             src = w1_raw[o][:].rearrange("p j (m t) -> p m j t", t=PACK)
@@ -97,13 +100,14 @@ def tile_picked_sub_mlp_silu_sub_p_kernel(
 
         def layer1(o, c):
             cols = slice(c * CHUNK, (c + 1) * CHUNK)
+            g, j0 = divmod(c * CHUNK, GATHER)
             for t in range(PACK):
                 ch = slice(t * P, (t + 1) * P)
                 nc.tensor.matmul_mx(
                     pre[c][:, t, :],
                     lhsT=w1_codes[o][:, ch].bitcast(FP8X4),
                     lhsT_scale=w1_scales[o][:, ch],
-                    rhs=x_codes[o][:, cols].bitcast(FP8X4),
+                    rhs=x_codes[o][g][:, j0 : j0 + CHUNK].bitcast(FP8X4),
                     rhs_scale=x_planes[4 * o :, cols],
                     start=(o == 0 and t == 0),
                     stop=(o == PASSES - 1 and t == PACK - 1),
@@ -121,18 +125,20 @@ def tile_picked_sub_mlp_silu_sub_p_kernel(
                 start=True,
                 stop=True,
             )
-            nc.vector.tensor_copy(y_sb[:, c * CHUNK : (c + 1) * CHUNK], y_ps[:])
+            if c == CHUNKS - 1:
+                nc.scalar.copy(y_sb[:, c * CHUNK : (c + 1) * CHUNK], y_ps[:])
+            else:
+                nc.vector.tensor_copy(y_sb[:, c * CHUNK : (c + 1) * CHUNK], y_ps[:])
 
         nc.vector.tensor_copy(x_planes[:], scales_all[:].bitcast(U8).indirect(offs_sb[:]))
         quantize_w1(0)
+        quantize_w1(1)
         for j0 in range(0, S, GATHER):
             gather_words(0, j0, GATHER)
-        for c in range(CHUNKS):
-            layer1(0, c)
-        quantize_w1(1)
         for j0 in range(0, S, GATHER):
             gather_words(1, j0, GATHER)
         for c in range(CHUNKS):
+            layer1(0, c)
             layer1(1, c)
             nc.scalar.activation(
                 h_bf[c][:].rearrange("p (n t) -> p n t", t=PACK), pre[c][:].rearrange("p t n -> p n t"), SILU

@@ -23,8 +23,10 @@ CHUNK = 128
 CHUNKS = S // CHUNK
 GATHER = 256
 STRIPE = 16
-M_SCALAR = (96, 96)
-V_PIECES = 2
+T_SCALAR = (3, 2)
+GROUPS = ((0, 2), (2, 4), (4, 5), (5, 6))
+RUN = 4
+V_PIECES = ((0, 256), (256, 384))
 
 
 def tile_picked_sub_mlp_silu_sub_p_kernel(
@@ -34,7 +36,6 @@ def tile_picked_sub_mlp_silu_sub_p_kernel(
     with ExitStack() as ctx:
         keep = ctx.enter_context(tc.tile_pool(name="keep", bufs=1))
         psum = ctx.enter_context(tc.psum_pool(name="psum", bufs=1))
-        psum_y = ctx.enter_context(tc.psum_pool(name="psum_y", bufs=2))
 
         offs_sb = keep.tile([P, S // STRIPE], U16, name="offs_sb")
         pos_sb = [keep.tile([P, V // STRIPE], U16, name=f"pos_sb{d}") for d in range(D)]
@@ -55,18 +56,23 @@ def tile_picked_sub_mlp_silu_sub_p_kernel(
 
         nc.vector.memset(scales_all[:], 0)
         nc.sync.dma_start(offs_sb[:], offs)
-        load_w1(0)
-        nc.sync.dma_start(pos_sb[0][:], pos1)
-        nc.sync.dma_start(pos_sb[1][:], pos2)
-        for q in range(4):
+        for q in range(2):
             nc.sync.dma_start(scales_all[32 * q : 32 * q + 8, :], x_scales[:, 4 * q : 4 * q + 4, :].bitcast(I32))
+        for q in range(2, 4):
+            for o in range(PASSES):
+                p0 = 32 * q + 4 * o
+                nc.sync.dma_start(scales_all[p0 : p0 + 4, :], x_scales[o, 4 * q : 4 * q + 4, :].bitcast(I32))
         nc.vector.memset(warm_in[:], 0.0)
         nc.scalar.activation(warm_out[:], warm_in[:], SILU)
-        load_w1(1)
+        load_w1(0)
         load_words(0)
+        load_w1(1)
         load_words(1)
-        nc.sync.dma_start(w2_raw[:], w2.rearrange("(p j) m -> p j m", j=PACK))
+        for t in range(PACK):
+            nc.sync.dma_start(w2_raw[:, t, :], w2.rearrange("(c t r) m -> t c r m", t=PACK, r=RUN)[t])
         nc.sync.dma_start(gate_sb[:], gate.rearrange("d m v -> m d v"))
+        nc.sync.dma_start(pos_sb[0][:], pos1)
+        nc.sync.dma_start(pos_sb[1][:], pos2)
 
         x_codes = [
             [keep.tile([P, GATHER], U32, name=f"x_codes{o}_{g}", align_bytes=64) for g in range(S // GATHER)]
@@ -80,9 +86,10 @@ def tile_picked_sub_mlp_silu_sub_p_kernel(
         w2_codes = keep.tile([P, N], U32, name="w2_codes", align_bytes=64)
         w2_scales = keep.tile([P, N], U8, name="w2_scales", align_bytes=64)
         pre = [psum.tile([P, PACK, CHUNK], F32, name=f"pre{c}") for c in range(CHUNKS)]
-        h_bf = [keep.tile([P, CHUNK * PACK], BF16, name=f"h_bf{c}", align_bytes=64) for c in range(CHUNKS)]
-        h_codes = [keep.tile([P, CHUNK], U32, name=f"h_codes{c}", align_bytes=64) for c in range(CHUNKS)]
-        h_scales = [keep.tile([P, CHUNK], U8, name=f"h_scales{c}", align_bytes=64) for c in range(CHUNKS)]
+        widths = [(c1 - c0) * CHUNK for c0, c1 in GROUPS]
+        h_bf = [keep.tile([P, n * PACK], BF16, name=f"h_bf{g}", align_bytes=64) for g, n in enumerate(widths)]
+        h_codes = [keep.tile([P, n], U32, name=f"h_codes{g}", align_bytes=64) for g, n in enumerate(widths)]
+        h_scales = [keep.tile([P, n], U8, name=f"h_scales{g}", align_bytes=64) for g, n in enumerate(widths)]
         y_sb = keep.tile([P, S], F32, name="y_sb")
 
         def gather_words(o, j0, n):
@@ -90,13 +97,20 @@ def tile_picked_sub_mlp_silu_sub_p_kernel(
             nc.vector.tensor_copy(x_codes[o][j0 // GATHER][:], words_all[o][:].bitcast(U32).indirect(entries))
 
         def quantize_w1(o):
-            src = w1_raw[o][:].rearrange("p j (m t) -> p m j t", t=PACK)
-            dst = w1_bf[o][:].rearrange("p (t m j) -> p m j t", t=PACK, j=PACK)
-            split = M_SCALAR[o]
-            nc.scalar.copy(dst[:, :split], src[:, :split])
-            if split < P:
-                nc.vector.tensor_copy(dst[:, split:], src[:, split:])
-            nc.vector.quantize_mx(w1_codes[o][:].bitcast(FP8X4), w1_scales[o][:], w1_bf[o][:])
+            src = w1_raw[o][:].rearrange("p j (c t r) -> p t c j r", t=PACK, r=RUN)
+            dst = w1_bf[o][:].rearrange("p (t c r j) -> p t c j r", t=PACK, r=RUN, j=PACK)
+            for t in range(PACK):
+                if t < T_SCALAR[o]:
+                    nc.scalar.copy(dst[:, t], src[:, t])
+                else:
+                    nc.vector.tensor_copy(dst[:, t], src[:, t])
+            for t in range(PACK):
+                ch = slice(t * P, (t + 1) * P)
+                nc.vector.quantize_mx(
+                    w1_codes[o][:, ch].bitcast(FP8X4),
+                    w1_scales[o][:, ch],
+                    w1_bf[o][:, t * P * PACK : (t + 1) * P * PACK],
+                )
 
         def layer1(o, c):
             cols = slice(c * CHUNK, (c + 1) * CHUNK)
@@ -113,46 +127,50 @@ def tile_picked_sub_mlp_silu_sub_p_kernel(
                     stop=(o == PASSES - 1 and t == PACK - 1),
                 )
 
-        def layer2(c):
-            nc.vector.quantize_mx(h_codes[c][:].bitcast(FP8X4), h_scales[c][:], h_bf[c][:])
-            y_ps = psum_y.tile([P, CHUNK], F32, name="y_ps")
+        def layer2(g):
+            c0, c1 = GROUPS[g]
+            nc.vector.quantize_mx(h_codes[g][:].bitcast(FP8X4), h_scales[g][:], h_bf[g][:])
+            y_ps = psum.tile([P, widths[g]], F32, name=f"y_ps{g}", tag=f"y_ps{g % 2}")
             nc.tensor.matmul_mx(
                 y_ps[:],
                 lhsT=w2_codes[:].bitcast(FP8X4),
                 lhsT_scale=w2_scales[:],
-                rhs=h_codes[c][:].bitcast(FP8X4),
-                rhs_scale=h_scales[c][:],
+                rhs=h_codes[g][:].bitcast(FP8X4),
+                rhs_scale=h_scales[g][:],
                 start=True,
                 stop=True,
             )
-            if c == CHUNKS - 1:
-                nc.scalar.copy(y_sb[:, c * CHUNK : (c + 1) * CHUNK], y_ps[:])
+            if g == len(GROUPS) - 1:
+                nc.scalar.copy(y_sb[:, c0 * CHUNK : c1 * CHUNK], y_ps[:])
             else:
-                nc.vector.tensor_copy(y_sb[:, c * CHUNK : (c + 1) * CHUNK], y_ps[:])
+                nc.vector.tensor_copy(y_sb[:, c0 * CHUNK : c1 * CHUNK], y_ps[:])
 
         nc.vector.tensor_copy(x_planes[:], scales_all[:].bitcast(U8).indirect(offs_sb[:]))
         quantize_w1(0)
-        quantize_w1(1)
         for j0 in range(0, S, GATHER):
             gather_words(0, j0, GATHER)
-        for j0 in range(0, S, GATHER):
-            gather_words(1, j0, GATHER)
         for c in range(CHUNKS):
             layer1(0, c)
-            layer1(1, c)
-            nc.scalar.activation(
-                h_bf[c][:].rearrange("p (n t) -> p n t", t=PACK), pre[c][:].rearrange("p t n -> p n t"), SILU
-            )
+        quantize_w1(1)
+        for j0 in range(0, S, GATHER):
+            gather_words(1, j0, GATHER)
         nc.vector.tensor_copy(
             w2_bf[:].rearrange("p (m j) -> p m j", j=PACK), w2_raw[:].rearrange("p j m -> p m j")
         )
         nc.vector.quantize_mx(w2_codes[:].bitcast(FP8X4), w2_scales[:], w2_bf[:])
-        for c in range(CHUNKS):
-            layer2(c)
+        for g, (c0, c1) in enumerate(GROUPS):
+            for c in range(c0, c1):
+                layer1(1, c)
+                h_out = h_bf[g][:, (c - c0) * CHUNK * PACK : (c - c0 + 1) * CHUNK * PACK]
+                nc.scalar.activation(
+                    h_out.rearrange("p (n t) -> p n t", t=PACK), pre[c][:].rearrange("p t n -> p n t"), SILU
+                )
+        for g in range(len(GROUPS)):
+            layer2(g)
 
-        width = V // V_PIECES
-        for i in range(V_PIECES):
-            cols = slice(i * width, (i + 1) * width)
+        for i, (v0, v1) in enumerate(V_PIECES):
+            cols = slice(v0, v1)
+            width = v1 - v0
             terms = []
             for d in range(D):
                 term = keep.tile([P, width], F32, name=f"term{i}_{d}")

@@ -23,6 +23,7 @@ CHUNK = 128
 CHUNKS = S // CHUNK
 GATHER = 256
 STRIPE = 16
+EARLY = 512
 T_SCALAR = (3, 2)
 GROUPS = ((0, 2), (2, 4), (4, 5), (5, 6))
 RUN = 4
@@ -39,9 +40,9 @@ def tile_picked_sub_mlp_silu_sub_p_kernel(
 
         offs_sb = keep.tile([P, S // STRIPE], U16, name="offs_sb")
         pos_sb = [keep.tile([P, V // STRIPE], U16, name=f"pos_sb{d}") for d in range(D)]
-        words_all = [keep.tile([P, T], I32, name=f"words_all{o}", align_bytes=64) for o in range(PASSES)]
-        scales_all = keep.tile([P, T // 4], I32, name="scales_all", align_bytes=64)
-        w1_raw = [keep.tile([P, PACK, H], F32, name=f"w1_raw{o}") for o in range(PASSES)]
+        words_all = [keep.tile([P, T], I32, name=f"words_all{o}", tag=f"words{o}", align_bytes=64) for o in range(PASSES)]
+        scales_all = keep.tile([P, T // 4], I32, name="scales_all", tag="scales", align_bytes=64)
+        w1_raw = [keep.tile([P, PACK, H], F32, name=f"w1_raw{o}", tag=f"raw{o}", align_bytes=64) for o in range(PASSES)]
         w2_raw = keep.tile([P, PACK, N], F32, name="w2_raw")
         gate_sb = keep.tile([P, D, V], F32, name="gate_sb")
         warm_in = keep.tile([P, 1], F32, name="warm_in")
@@ -56,6 +57,7 @@ def tile_picked_sub_mlp_silu_sub_p_kernel(
 
         nc.vector.memset(scales_all[:], 0)
         nc.sync.dma_start(offs_sb[:], offs)
+        load_w1(0)
         for q in range(2):
             nc.sync.dma_start(scales_all[32 * q : 32 * q + 8, :], x_scales[:, 4 * q : 4 * q + 4, :].bitcast(I32))
         for q in range(2, 4):
@@ -64,7 +66,6 @@ def tile_picked_sub_mlp_silu_sub_p_kernel(
                 nc.sync.dma_start(scales_all[p0 : p0 + 4, :], x_scales[o, 4 * q : 4 * q + 4, :].bitcast(I32))
         nc.vector.memset(warm_in[:], 0.0)
         nc.scalar.activation(warm_out[:], warm_in[:], SILU)
-        load_w1(0)
         load_words(0)
         load_w1(1)
         load_words(1)
@@ -74,15 +75,13 @@ def tile_picked_sub_mlp_silu_sub_p_kernel(
         nc.sync.dma_start(pos_sb[0][:], pos1)
         nc.sync.dma_start(pos_sb[1][:], pos2)
 
-        x_codes = [
-            [keep.tile([P, GATHER], U32, name=f"x_codes{o}_{g}", align_bytes=64) for g in range(S // GATHER)]
-            for o in range(PASSES)
-        ]
+        x_codes = {}
         x_planes = keep.tile([P, S], U8, name="x_planes", align_bytes=64)
-        w1_bf = [keep.tile([P, H * PACK], BF16, name=f"w1_bf{o}", align_bytes=64) for o in range(PASSES)]
-        w1_codes = [keep.tile([P, H], U32, name=f"w1_codes{o}", align_bytes=64) for o in range(PASSES)]
+        w1_bf = [
+            keep.tile([P, H * PACK], BF16, name=f"w1_bf{o}", tag=f"pass{o}", align_bytes=64) for o in range(PASSES)
+        ]
+        w1_codes = {}
         w1_scales = [keep.tile([P, H], U8, name=f"w1_scales{o}", align_bytes=64) for o in range(PASSES)]
-        w2_bf = keep.tile([P, N * PACK], BF16, name="w2_bf", align_bytes=64)
         w2_codes = keep.tile([P, N], U32, name="w2_codes", align_bytes=64)
         w2_scales = keep.tile([P, N], U8, name="w2_scales", align_bytes=64)
         pre = [psum.tile([P, PACK, CHUNK], F32, name=f"pre{c}") for c in range(CHUNKS)]
@@ -92,11 +91,17 @@ def tile_picked_sub_mlp_silu_sub_p_kernel(
         h_scales = [keep.tile([P, n], U8, name=f"h_scales{g}", align_bytes=64) for g, n in enumerate(widths)]
         y_sb = keep.tile([P, S], F32, name="y_sb")
 
-        def gather_words(o, j0, n):
-            entries = offs_sb[:, j0 // STRIPE : (j0 + n) // STRIPE]
-            nc.vector.tensor_copy(x_codes[o][j0 // GATHER][:], words_all[o][:].bitcast(U32).indirect(entries))
+        def gather_words(o, j0, j1, tag):
+            codes = keep.tile([P, j1 - j0], U32, name=f"x_codes{o}_{j0}", tag=tag, align_bytes=64)
+            for j in range(j0, j1, GATHER):
+                entries = offs_sb[:, j // STRIPE : (j + GATHER) // STRIPE]
+                nc.vector.tensor_copy(
+                    codes[:, j - j0 : j - j0 + GATHER], words_all[o][:].bitcast(U32).indirect(entries)
+                )
+            for j in range(j0, j1, CHUNK):
+                x_codes[o, j // CHUNK] = codes[:, j - j0 : j - j0 + CHUNK]
 
-        def quantize_w1(o):
+        def cast_w1(o):
             src = w1_raw[o][:].rearrange("p j (c t r) -> p t c j r", t=PACK, r=RUN)
             dst = w1_bf[o][:].rearrange("p (t c r j) -> p t c j r", t=PACK, r=RUN, j=PACK)
             for t in range(PACK):
@@ -104,6 +109,11 @@ def tile_picked_sub_mlp_silu_sub_p_kernel(
                     nc.scalar.copy(dst[:, t], src[:, t])
                 else:
                     nc.vector.tensor_copy(dst[:, t], src[:, t])
+
+        def quantize_w1(o):
+            w1_codes[o] = keep.tile(
+                [P, H], U32, name=f"w1_codes{o}", tag=("scales", "codes1")[o], align_bytes=64
+            )
             for t in range(PACK):
                 ch = slice(t * P, (t + 1) * P)
                 nc.vector.quantize_mx(
@@ -114,14 +124,13 @@ def tile_picked_sub_mlp_silu_sub_p_kernel(
 
         def layer1(o, c):
             cols = slice(c * CHUNK, (c + 1) * CHUNK)
-            g, j0 = divmod(c * CHUNK, GATHER)
             for t in range(PACK):
                 ch = slice(t * P, (t + 1) * P)
                 nc.tensor.matmul_mx(
                     pre[c][:, t, :],
                     lhsT=w1_codes[o][:, ch].bitcast(FP8X4),
                     lhsT_scale=w1_scales[o][:, ch],
-                    rhs=x_codes[o][g][:, j0 : j0 + CHUNK].bitcast(FP8X4),
+                    rhs=x_codes[o, c].bitcast(FP8X4),
                     rhs_scale=x_planes[4 * o :, cols],
                     start=(o == 0 and t == 0),
                     stop=(o == PASSES - 1 and t == PACK - 1),
@@ -146,14 +155,16 @@ def tile_picked_sub_mlp_silu_sub_p_kernel(
                 nc.vector.tensor_copy(y_sb[:, c0 * CHUNK : c1 * CHUNK], y_ps[:])
 
         nc.vector.tensor_copy(x_planes[:], scales_all[:].bitcast(U8).indirect(offs_sb[:]))
+        cast_w1(0)
         quantize_w1(0)
-        for j0 in range(0, S, GATHER):
-            gather_words(0, j0, GATHER)
+        gather_words(0, 0, EARLY, "pass0")
+        cast_w1(1)
+        gather_words(0, EARLY, S, "raw1")
         for c in range(CHUNKS):
             layer1(0, c)
         quantize_w1(1)
-        for j0 in range(0, S, GATHER):
-            gather_words(1, j0, GATHER)
+        gather_words(1, 0, S, "pass1")
+        w2_bf = keep.tile([P, N * PACK], BF16, name="w2_bf", tag="words1", align_bytes=64)
         nc.vector.tensor_copy(
             w2_bf[:].rearrange("p (m j) -> p m j", j=PACK), w2_raw[:].rearrange("p j m -> p m j")
         )
@@ -168,15 +179,15 @@ def tile_picked_sub_mlp_silu_sub_p_kernel(
         for g in range(len(GROUPS)):
             layer2(g)
 
+        first = keep.tile([P, V], F32, name="first")
+        nc.vector.tensor_tensor(first[:], y_sb[:].indirect(pos_sb[0][:]), gate_sb[:, 0, :], MULT)
+        second = []
         for i, (v0, v1) in enumerate(V_PIECES):
-            cols = slice(v0, v1)
-            width = v1 - v0
-            terms = []
-            for d in range(D):
-                term = keep.tile([P, width], F32, name=f"term{i}_{d}")
-                entries = pos_sb[d][:, cols.start // STRIPE : cols.stop // STRIPE]
-                nc.vector.tensor_tensor(term[:], y_sb[:].indirect(entries), gate_sb[:, d, cols], MULT)
-                terms.append(term)
-            res = keep.tile([P, width], F32, name=f"res{i}")
-            nc.vector.tensor_add(res[:], terms[0][:], terms[1][:])
-            nc.sync.dma_start(out[:, cols], res[:])
+            term = keep.tile([P, v1 - v0], F32, name=f"second{i}")
+            entries = pos_sb[1][:, v0 // STRIPE : v1 // STRIPE]
+            nc.vector.tensor_tensor(term[:], y_sb[:].indirect(entries), gate_sb[:, 1, v0:v1], MULT)
+            second.append(term)
+        for i, (v0, v1) in enumerate(V_PIECES):
+            res = keep.tile([P, v1 - v0], F32, name=f"res{i}")
+            nc.vector.tensor_add(res[:], first[:, v0:v1], second[i][:])
+            nc.sync.dma_start(out[:, v0:v1], res[:])

@@ -19,14 +19,18 @@ P = 128
 PACK = 4
 K_PASS = P * PACK
 PASSES = K // K_PASS
+QUADRANT = 32
+QUADRANTS = P // QUADRANT
+SCALE_ROWS = 4
+STRIPE = 16
+RUN = 4
 CHUNK = 128
 CHUNKS = S // CHUNK
 GATHER = 256
-STRIPE = 16
+JOINT_QUADRANTS = 2
 EARLY = 512
-T_SCALAR = (3, 2)
+SCALAR_PLANES = (3, 2)
 GROUPS = ((0, 2), (2, 4), (4, 5), (5, 6))
-RUN = 4
 V_PIECES = ((0, 256), (256, 384))
 
 
@@ -40,13 +44,17 @@ def tile_picked_sub_mlp_silu_sub_p_kernel(
 
         offs_sb = keep.tile([P, S // STRIPE], U16, name="offs_sb")
         pos_sb = [keep.tile([P, V // STRIPE], U16, name=f"pos_sb{d}") for d in range(D)]
-        words_all = [keep.tile([P, T], I32, name=f"words_all{o}", tag=f"words{o}", align_bytes=64) for o in range(PASSES)]
-        scales_all = keep.tile([P, T // 4], I32, name="scales_all", tag="scales", align_bytes=64)
-        w1_raw = [keep.tile([P, PACK, H], F32, name=f"w1_raw{o}", tag=f"raw{o}", align_bytes=64) for o in range(PASSES)]
+        words_all = [
+            keep.tile([P, T], I32, name=f"words_all{o}", tag=f"words{o}", align_bytes=64) for o in range(PASSES)
+        ]
+        scales_all = keep.tile([P, T // PACK], I32, name="scales_all", tag="scales", align_bytes=64)
+        w1_raw = [
+            keep.tile([P, PACK, H], F32, name=f"w1_raw{o}", tag=f"raw{o}", align_bytes=64) for o in range(PASSES)
+        ]
         w2_raw = keep.tile([P, PACK, N], F32, name="w2_raw")
         gate_sb = keep.tile([P, D, V], F32, name="gate_sb")
-        warm_in = keep.tile([P, 1], F32, name="warm_in")
-        warm_out = keep.tile([P, 1], F32, name="warm_out")
+        zero = keep.tile([P, 1], F32, name="zero")
+        silu_bias = keep.tile([P, 1], F32, name="silu_bias")
 
         def load_words(o):
             nc.sync.dma_start(words_all[o][:], x_words[o].rearrange("p n t -> p (n t)").bitcast(I32))
@@ -58,27 +66,30 @@ def tile_picked_sub_mlp_silu_sub_p_kernel(
         nc.vector.memset(scales_all[:], 0)
         nc.sync.dma_start(offs_sb[:], offs)
         load_w1(0)
-        for q in range(2):
-            nc.sync.dma_start(scales_all[32 * q : 32 * q + 8, :], x_scales[:, 4 * q : 4 * q + 4, :].bitcast(I32))
-        for q in range(2, 4):
-            for o in range(PASSES):
-                p0 = 32 * q + 4 * o
-                nc.sync.dma_start(scales_all[p0 : p0 + 4, :], x_scales[o, 4 * q : 4 * q + 4, :].bitcast(I32))
-        nc.vector.memset(warm_in[:], 0.0)
-        nc.scalar.activation(warm_out[:], warm_in[:], SILU)
+        for q in range(QUADRANTS):
+            rows = slice(SCALE_ROWS * q, SCALE_ROWS * (q + 1))
+            p0 = QUADRANT * q
+            if q < JOINT_QUADRANTS:
+                nc.sync.dma_start(scales_all[p0 : p0 + PASSES * SCALE_ROWS, :], x_scales[:, rows, :].bitcast(I32))
+            else:
+                for o in range(PASSES):
+                    p1 = p0 + SCALE_ROWS * o
+                    nc.sync.dma_start(scales_all[p1 : p1 + SCALE_ROWS, :], x_scales[o, rows, :].bitcast(I32))
+        nc.vector.memset(zero[:], 0.0)
+        nc.scalar.activation(silu_bias[:], zero[:], SILU)
         load_words(0)
         load_w1(1)
         load_words(1)
         for t in range(PACK):
-            nc.sync.dma_start(w2_raw[:, t, :], w2.rearrange("(c t r) m -> t c r m", t=PACK, r=RUN)[t])
+            nc.sync.dma_start(w2_raw[:, t, :], w2.rearrange("(a t r) m -> t a r m", t=PACK, r=RUN)[t])
         nc.sync.dma_start(gate_sb[:], gate.rearrange("d m v -> m d v"))
         nc.sync.dma_start(pos_sb[0][:], pos1)
         nc.sync.dma_start(pos_sb[1][:], pos2)
 
         x_codes = {}
-        x_planes = keep.tile([P, S], U8, name="x_planes", align_bytes=64)
+        scales_picked = keep.tile([P, S], U8, name="scales_picked", align_bytes=64)
         w1_bf = [
-            keep.tile([P, H * PACK], BF16, name=f"w1_bf{o}", tag=f"pass{o}", align_bytes=64) for o in range(PASSES)
+            keep.tile([P, H * PACK], BF16, name=f"w1_bf{o}", tag=f"bf{o}", align_bytes=64) for o in range(PASSES)
         ]
         w1_codes = {}
         w1_scales = [keep.tile([P, H], U8, name=f"w1_scales{o}", align_bytes=64) for o in range(PASSES)]
@@ -102,36 +113,34 @@ def tile_picked_sub_mlp_silu_sub_p_kernel(
                 x_codes[o, j // CHUNK] = codes[:, j - j0 : j - j0 + CHUNK]
 
         def cast_w1(o):
-            src = w1_raw[o][:].rearrange("p j (c t r) -> p t c j r", t=PACK, r=RUN)
-            dst = w1_bf[o][:].rearrange("p (t c r j) -> p t c j r", t=PACK, r=RUN, j=PACK)
+            src = w1_raw[o][:].rearrange("p j (a t r) -> p t a j r", t=PACK, r=RUN)
+            dst = w1_bf[o][:].rearrange("p (t a r j) -> p t a j r", t=PACK, r=RUN, j=PACK)
             for t in range(PACK):
-                if t < T_SCALAR[o]:
+                if t < SCALAR_PLANES[o]:
                     nc.scalar.copy(dst[:, t], src[:, t])
                 else:
                     nc.vector.tensor_copy(dst[:, t], src[:, t])
 
-        def quantize_w1(o):
-            w1_codes[o] = keep.tile(
-                [P, H], U32, name=f"w1_codes{o}", tag=("scales", "codes1")[o], align_bytes=64
-            )
+        def quantize_w1(o, tag):
+            w1_codes[o] = keep.tile([P, H], U32, name=f"w1_codes{o}", tag=tag, align_bytes=64)
             for t in range(PACK):
-                ch = slice(t * P, (t + 1) * P)
+                plane = slice(t * P, (t + 1) * P)
                 nc.vector.quantize_mx(
-                    w1_codes[o][:, ch].bitcast(FP8X4),
-                    w1_scales[o][:, ch],
+                    w1_codes[o][:, plane].bitcast(FP8X4),
+                    w1_scales[o][:, plane],
                     w1_bf[o][:, t * P * PACK : (t + 1) * P * PACK],
                 )
 
         def layer1(o, c):
-            cols = slice(c * CHUNK, (c + 1) * CHUNK)
+            nodes = slice(c * CHUNK, (c + 1) * CHUNK)
             for t in range(PACK):
-                ch = slice(t * P, (t + 1) * P)
+                plane = slice(t * P, (t + 1) * P)
                 nc.tensor.matmul_mx(
                     pre[c][:, t, :],
-                    lhsT=w1_codes[o][:, ch].bitcast(FP8X4),
-                    lhsT_scale=w1_scales[o][:, ch],
+                    lhsT=w1_codes[o][:, plane].bitcast(FP8X4),
+                    lhsT_scale=w1_scales[o][:, plane],
                     rhs=x_codes[o, c].bitcast(FP8X4),
-                    rhs_scale=x_planes[4 * o :, cols],
+                    rhs_scale=scales_picked[SCALE_ROWS * o :, nodes],
                     start=(o == 0 and t == 0),
                     stop=(o == PASSES - 1 and t == PACK - 1),
                 )
@@ -154,19 +163,20 @@ def tile_picked_sub_mlp_silu_sub_p_kernel(
             else:
                 nc.vector.tensor_copy(y_sb[:, c0 * CHUNK : c1 * CHUNK], y_ps[:])
 
-        nc.vector.tensor_copy(x_planes[:], scales_all[:].bitcast(U8).indirect(offs_sb[:]))
+        nc.vector.tensor_copy(scales_picked[:], scales_all[:].bitcast(U8).indirect(offs_sb[:]))
         cast_w1(0)
-        quantize_w1(0)
-        gather_words(0, 0, EARLY, "pass0")
+        quantize_w1(0, "scales")
+        gather_words(0, 0, EARLY, "bf0")
         cast_w1(1)
         gather_words(0, EARLY, S, "raw1")
         for c in range(CHUNKS):
             layer1(0, c)
-        quantize_w1(1)
-        gather_words(1, 0, S, "pass1")
+
+        quantize_w1(1, "codes1")
+        gather_words(1, 0, S, "bf1")
         w2_bf = keep.tile([P, N * PACK], BF16, name="w2_bf", tag="words1", align_bytes=64)
         nc.vector.tensor_copy(
-            w2_bf[:].rearrange("p (m j) -> p m j", j=PACK), w2_raw[:].rearrange("p j m -> p m j")
+            w2_bf[:].rearrange("p (m t) -> p m t", t=PACK), w2_raw[:].rearrange("p t m -> p m t")
         )
         nc.vector.quantize_mx(w2_codes[:].bitcast(FP8X4), w2_scales[:], w2_bf[:])
         for g, (c0, c1) in enumerate(GROUPS):
@@ -174,7 +184,10 @@ def tile_picked_sub_mlp_silu_sub_p_kernel(
                 layer1(1, c)
                 h_out = h_bf[g][:, (c - c0) * CHUNK * PACK : (c - c0 + 1) * CHUNK * PACK]
                 nc.scalar.activation(
-                    h_out.rearrange("p (n t) -> p n t", t=PACK), pre[c][:].rearrange("p t n -> p n t"), SILU
+                    h_out.rearrange("p (n t) -> p n t", t=PACK),
+                    pre[c][:].rearrange("p t n -> p n t"),
+                    SILU,
+                    bias=silu_bias[:],
                 )
         for g in range(len(GROUPS)):
             layer2(g)

@@ -30,7 +30,7 @@ GATHER = 256
 JOINT_QUADRANTS = 2
 EARLY = 512
 SCALAR_PLANES = (3, 2)
-GROUPS = ((0, 2), (2, 4), (4, 5), (5, 6))
+GROUPS = ((0, 256), (256, 512), (512, 640), (640, 704), (704, 768))
 V_PIECES = ((0, 256), (256, 384))
 
 
@@ -44,59 +44,61 @@ def tile_picked_sub_mlp_silu_sub_p_kernel(
 
         offs_sb = keep.tile([P, S // STRIPE], U16, name="offs_sb")
         pos_sb = [keep.tile([P, V // STRIPE], U16, name=f"pos_sb{d}") for d in range(D)]
-        words_all = [
-            keep.tile([P, T], I32, name=f"words_all{o}", tag=f"words{o}", align_bytes=64) for o in range(PASSES)
-        ]
+        words_all = {}
+        scales_picked = keep.tile([P, S], U8, name="scales_picked", align_bytes=64)
+        planes = {}
         scales_all = keep.tile([P, T // PACK], I32, name="scales_all", tag="scales", align_bytes=64)
-        w1_raw = [
-            keep.tile([P, PACK, H], F32, name=f"w1_raw{o}", tag=f"raw{o}", align_bytes=64) for o in range(PASSES)
-        ]
-        w2_raw = keep.tile([P, PACK, N], F32, name="w2_raw")
-        gate_sb = keep.tile([P, D, V], F32, name="gate_sb")
+        w1_raw = {}
         zero = keep.tile([P, 1], F32, name="zero")
         silu_bias = keep.tile([P, 1], F32, name="silu_bias")
 
-        def load_words(o):
+        def load_words(o, tag):
+            words_all[o] = keep.tile([P, T], I32, name=f"words_all{o}", tag=tag, align_bytes=64)
             nc.sync.dma_start(words_all[o][:], x_words[o].rearrange("p n t -> p (n t)").bitcast(I32))
 
-        def load_w1(o):
+        def load_w1(o, tag):
+            w1_raw[o] = keep.tile([P, PACK, H], F32, name=f"w1_raw{o}", tag=tag, align_bytes=64)
             rows = w1[o * K_PASS : (o + 1) * K_PASS, :]
             nc.sync.dma_start(w1_raw[o][:], rows.rearrange("(p j) c -> p j c", j=PACK))
 
-        nc.vector.memset(scales_all[:], 0)
         nc.sync.dma_start(offs_sb[:], offs)
-        load_w1(0)
-        for q in range(QUADRANTS):
-            rows = slice(SCALE_ROWS * q, SCALE_ROWS * (q + 1))
-            p0 = QUADRANT * q
-            if q < JOINT_QUADRANTS:
-                nc.sync.dma_start(scales_all[p0 : p0 + PASSES * SCALE_ROWS, :], x_scales[:, rows, :].bitcast(I32))
-            else:
-                for o in range(PASSES):
-                    p1 = p0 + SCALE_ROWS * o
-                    nc.sync.dma_start(scales_all[p1 : p1 + SCALE_ROWS, :], x_scales[o, rows, :].bitcast(I32))
-        nc.vector.memset(zero[:], 0.0)
-        nc.scalar.activation(silu_bias[:], zero[:], SILU)
-        load_words(0)
-        load_w1(1)
-        load_words(1)
-        for t in range(PACK):
-            nc.sync.dma_start(w2_raw[:, t, :], w2.rearrange("(a t r) m -> t a r m", t=PACK, r=RUN)[t])
-        nc.sync.dma_start(gate_sb[:], gate.rearrange("d m v -> m d v"))
+        nc.sync.dma_start(scales_all[:QUADRANT, :], x_scales.rearrange("o q n -> (o q) n").bitcast(I32))
+        nc.vector.memset(scales_all[QUADRANT : 2 * QUADRANT, :], 0)
+        nc.vector.memset(scales_all[2 * QUADRANT :, :], 0)
+        load_w1(0, "raw0")
         nc.sync.dma_start(pos_sb[0][:], pos1)
         nc.sync.dma_start(pos_sb[1][:], pos2)
+        nc.vector.memset(zero[:], 0.0)
+        nc.scalar.activation(silu_bias[:], zero[:], SILU)
+        load_words(0, "words0")
+        nc.vector.tensor_copy(scales_picked[:], scales_all[:].bitcast(U8).indirect(offs_sb[:]))
+
+        def move_scales(o, tag):
+            planes[o] = keep.tile([P, S], U8, name=f"planes{o}", tag=tag, align_bytes=64)
+            nc.vector.memset(planes[o][:].bitcast(I32), 0)
+            for q in range(QUADRANTS):
+                src = (o * QUADRANTS + q) * SCALE_ROWS
+                dst = QUADRANT * q + SCALE_ROWS * o
+                nc.sync.dma_start(
+                    planes[o][dst : dst + SCALE_ROWS, :].bitcast(I32),
+                    scales_picked[src : src + SCALE_ROWS, :].bitcast(I32),
+                )
+
+        move_scales(0, "planes0")
+        load_w1(1, "scales")
 
         x_codes = {}
-        scales_picked = keep.tile([P, S], U8, name="scales_picked", align_bytes=64)
-        w1_bf = [
-            keep.tile([P, H * PACK], BF16, name=f"w1_bf{o}", tag=f"bf{o}", align_bytes=64) for o in range(PASSES)
-        ]
+        w1_bf = {
+            (o, u): keep.tile([P, H * PACK // 2], BF16, name=f"w1_bf{o}{u}", tag=f"bf{o}{u}", align_bytes=64)
+            for o in range(PASSES)
+            for u in range(2)
+        }
         w1_codes = {}
         w1_scales = [keep.tile([P, H], U8, name=f"w1_scales{o}", align_bytes=64) for o in range(PASSES)]
         w2_codes = keep.tile([P, N], U32, name="w2_codes", align_bytes=64)
         w2_scales = keep.tile([P, N], U8, name="w2_scales", align_bytes=64)
-        pre = [psum.tile([P, PACK, CHUNK], F32, name=f"pre{c}") for c in range(CHUNKS)]
-        widths = [(c1 - c0) * CHUNK for c0, c1 in GROUPS]
+        pre = [psum.tile([P, PACK, CHUNK], F32, name=f"pre{c}", tag=f"bank{c}") for c in range(CHUNKS)]
+        widths = [j1 - j0 for j0, j1 in GROUPS]
         h_bf = [keep.tile([P, n * PACK], BF16, name=f"h_bf{g}", align_bytes=64) for g, n in enumerate(widths)]
         h_codes = [keep.tile([P, n], U32, name=f"h_codes{g}", align_bytes=64) for g, n in enumerate(widths)]
         h_scales = [keep.tile([P, n], U8, name=f"h_scales{g}", align_bytes=64) for g, n in enumerate(widths)]
@@ -113,13 +115,10 @@ def tile_picked_sub_mlp_silu_sub_p_kernel(
                 x_codes[o, j // CHUNK] = codes[:, j - j0 : j - j0 + CHUNK]
 
         def cast_w1(o):
-            src = w1_raw[o][:].rearrange("p j (a t r) -> p t a j r", t=PACK, r=RUN)
-            dst = w1_bf[o][:].rearrange("p (t a r j) -> p t a j r", t=PACK, r=RUN, j=PACK)
-            for t in range(PACK):
-                if t < SCALAR_PLANES[o]:
-                    nc.scalar.copy(dst[:, t], src[:, t])
-                else:
-                    nc.vector.tensor_copy(dst[:, t], src[:, t])
+            src = w1_raw[o][:].rearrange("p j (a u r v) -> p u a j r v", u=2, r=2, v=2)
+            dst = [w1_bf[o, u][:].rearrange("p (v a r j) -> p a j r v", v=2, r=2, j=PACK) for u in range(2)]
+            nc.vector.tensor_copy(dst[0], src[:, 0])
+            nc.scalar.copy(dst[1], src[:, 1])
 
         def quantize_w1(o, tag):
             w1_codes[o] = keep.tile([P, H], U32, name=f"w1_codes{o}", tag=tag, align_bytes=64)
@@ -128,7 +127,7 @@ def tile_picked_sub_mlp_silu_sub_p_kernel(
                 nc.vector.quantize_mx(
                     w1_codes[o][:, plane].bitcast(FP8X4),
                     w1_scales[o][:, plane],
-                    w1_bf[o][:, t * P * PACK : (t + 1) * P * PACK],
+                    w1_bf[o, t // 2][:, t % 2 * P * PACK : (t % 2 + 1) * P * PACK],
                 )
 
         def layer1(o, c):
@@ -140,15 +139,15 @@ def tile_picked_sub_mlp_silu_sub_p_kernel(
                     lhsT=w1_codes[o][:, plane].bitcast(FP8X4),
                     lhsT_scale=w1_scales[o][:, plane],
                     rhs=x_codes[o, c].bitcast(FP8X4),
-                    rhs_scale=scales_picked[SCALE_ROWS * o :, nodes],
+                    rhs_scale=planes[o][SCALE_ROWS * o :, nodes],
                     start=(o == 0 and t == 0),
                     stop=(o == PASSES - 1 and t == PACK - 1),
                 )
 
         def layer2(g):
-            c0, c1 = GROUPS[g]
+            j0, j1 = GROUPS[g]
             nc.vector.quantize_mx(h_codes[g][:].bitcast(FP8X4), h_scales[g][:], h_bf[g][:])
-            y_ps = psum.tile([P, widths[g]], F32, name=f"y_ps{g}", tag=f"y_ps{g % 2}")
+            y_ps = psum.tile([P, widths[g]], F32, name=f"y_ps{g}", tag=f"bank{(CHUNKS + g) % 8}")
             nc.tensor.matmul_mx(
                 y_ps[:],
                 lhsT=w2_codes[:].bitcast(FP8X4),
@@ -159,33 +158,43 @@ def tile_picked_sub_mlp_silu_sub_p_kernel(
                 stop=True,
             )
             if g == len(GROUPS) - 1:
-                nc.scalar.copy(y_sb[:, c0 * CHUNK : c1 * CHUNK], y_ps[:])
+                nc.scalar.copy(y_sb[:, j0:j1], y_ps[:])
             else:
-                nc.vector.tensor_copy(y_sb[:, c0 * CHUNK : c1 * CHUNK], y_ps[:])
+                nc.vector.tensor_copy(y_sb[:, j0:j1], y_ps[:])
 
-        nc.vector.tensor_copy(scales_picked[:], scales_all[:].bitcast(U8).indirect(offs_sb[:]))
         cast_w1(0)
-        quantize_w1(0, "scales")
-        gather_words(0, 0, EARLY, "bf0")
+        load_words(1, "raw0")
+        quantize_w1(0, "codes0")
+        move_scales(1, "bf01")
+        gather_words(0, 0, EARLY, "xc0")
         cast_w1(1)
-        gather_words(0, EARLY, S, "raw1")
+        quantize_w1(1, "codes1")
+        gather_words(0, EARLY, S, "bf10")
         for c in range(CHUNKS):
             layer1(0, c)
-
-        quantize_w1(1, "codes1")
-        gather_words(1, 0, S, "bf1")
-        w2_bf = keep.tile([P, N * PACK], BF16, name="w2_bf", tag="words1", align_bytes=64)
+        w2_raw = keep.tile([P, PACK, N], F32, name="w2_raw", tag="scales", align_bytes=64)
+        for u in range(2):
+            nc.sync.dma_start(
+                w2_raw[:, 2 * u : 2 * u + 2, :].rearrange("p v m -> p (v m)"),
+                w2.rearrange("(a u r v) m -> u a r (v m)", u=2, r=2, v=2)[u],
+            )
+        gather_words(1, 0, S, "xc1")
+        gate_sb = keep.tile([P, D, V], F32, name="gate_sb", tag="bf11", align_bytes=64)
+        nc.sync.dma_start(gate_sb[:], gate.rearrange("d m v -> m d v"))
+        w2_bf = keep.tile([P, N * PACK], BF16, name="w2_bf", tag="raw0", align_bytes=64)
         nc.vector.tensor_copy(
             w2_bf[:].rearrange("p (m t) -> p m t", t=PACK), w2_raw[:].rearrange("p t m -> p m t")
         )
         nc.vector.quantize_mx(w2_codes[:].bitcast(FP8X4), w2_scales[:], w2_bf[:])
-        for g, (c0, c1) in enumerate(GROUPS):
-            for c in range(c0, c1):
-                layer1(1, c)
-                h_out = h_bf[g][:, (c - c0) * CHUNK * PACK : (c - c0 + 1) * CHUNK * PACK]
+        for c in range(CHUNKS):
+            layer1(1, c)
+        for g, (j0, j1) in enumerate(GROUPS):
+            for j in range(j0, j1, CHUNK):
+                n = min(CHUNK, j1 - j)
+                h_out = h_bf[g][:, (j - j0) * PACK : (j - j0 + n) * PACK]
                 nc.scalar.activation(
                     h_out.rearrange("p (n t) -> p n t", t=PACK),
-                    pre[c][:].rearrange("p t n -> p n t"),
+                    pre[j // CHUNK][:, :, j % CHUNK : j % CHUNK + n].rearrange("p t n -> p n t"),
                     SILU,
                     bias=silu_bias[:],
                 )

@@ -62,7 +62,7 @@ def tile_picked_sub_mlp_silu_sub_p_kernel(
             nc.sync.dma_start(w1_raw[o][:], rows.rearrange("(p j) c -> p j c", j=PACK))
 
         nc.sync.dma_start(offs_sb[:], offs)
-        nc.sync.dma_start(scales_all[:QUADRANT, :], x_scales.rearrange("o q n -> (o q) n").bitcast(I32))
+        nc.scalar.dma_start(scales_all[:QUADRANT, :], x_scales.rearrange("o q n -> (o q) n").bitcast(I32))
         nc.vector.memset(scales_all[QUADRANT : 2 * QUADRANT, :], 0)
         nc.vector.memset(scales_all[2 * QUADRANT :, :], 0)
         load_w1(0, "raw0")
@@ -79,7 +79,8 @@ def tile_picked_sub_mlp_silu_sub_p_kernel(
             for q in range(QUADRANTS):
                 src = (o * QUADRANTS + q) * SCALE_ROWS
                 dst = QUADRANT * q + SCALE_ROWS * o
-                nc.sync.dma_start(
+                queue = nc.scalar if o == 0 and q % 2 else nc.sync
+                queue.dma_start(
                     planes[o][dst : dst + SCALE_ROWS, :].bitcast(I32),
                     scales_picked[src : src + SCALE_ROWS, :].bitcast(I32),
                 )
@@ -157,7 +158,7 @@ def tile_picked_sub_mlp_silu_sub_p_kernel(
                 start=True,
                 stop=True,
             )
-            if g == len(GROUPS) - 1:
+            if g in (1, len(GROUPS) - 1):
                 nc.scalar.copy(y_sb[:, j0:j1], y_ps[:])
             else:
                 nc.vector.tensor_copy(y_sb[:, j0:j1], y_ps[:])
@@ -166,12 +167,11 @@ def tile_picked_sub_mlp_silu_sub_p_kernel(
         load_words(1, "raw0")
         quantize_w1(0, "codes0")
         move_scales(1, "bf01")
-        gather_words(0, 0, EARLY, "xc0")
-        cast_w1(1)
-        quantize_w1(1, "codes1")
-        gather_words(0, EARLY, S, "bf10")
+        gather_words(0, 0, S, "xc0")
         for c in range(CHUNKS):
             layer1(0, c)
+        cast_w1(1)
+        quantize_w1(1, "codes1")
         w2_raw = keep.tile([P, PACK, N], F32, name="w2_raw", tag="scales", align_bytes=64)
         for u in range(2):
             nc.sync.dma_start(
@@ -186,7 +186,7 @@ def tile_picked_sub_mlp_silu_sub_p_kernel(
             w2_bf[:].rearrange("p (m t) -> p m t", t=PACK), w2_raw[:].rearrange("p t m -> p m t")
         )
         nc.vector.quantize_mx(w2_codes[:].bitcast(FP8X4), w2_scales[:], w2_bf[:])
-        for c in range(CHUNKS):
+        for c in (0, 1, 3, 2, 5, 4):
             layer1(1, c)
         for g, (j0, j1) in enumerate(GROUPS):
             for j in range(j0, j1, CHUNK):

@@ -158,7 +158,7 @@ def tile_picked_sub_mlp_silu_sub_p_kernel(
                 start=True,
                 stop=True,
             )
-            if g in (1, len(GROUPS) - 1):
+            if 0 < g < len(GROUPS) - 1:
                 nc.scalar.copy(y_sb[:, j0:j1], y_ps[:])
             else:
                 nc.vector.tensor_copy(y_sb[:, j0:j1], y_ps[:])

@@ -158,7 +158,9 @@ def tile_picked_sub_mlp_silu_sub_p_kernel(
                 start=True,
                 stop=True,
             )
-            if 0 < g < len(GROUPS) - 1:
+            if g == 1:
+                nc.scalar.activation(y_sb[:, j0:j1], y_ps[:], mybir.ActivationFunctionType.Identity, bias=silu_bias[:])
+            elif g > 1:
                 nc.scalar.copy(y_sb[:, j0:j1], y_ps[:])
             else:
                 nc.vector.tensor_copy(y_sb[:, j0:j1], y_ps[:])
@@ -196,7 +198,6 @@ def tile_picked_sub_mlp_silu_sub_p_kernel(
                     h_out.rearrange("p (n t) -> p n t", t=PACK),
                     pre[j // CHUNK][:, :, j % CHUNK : j % CHUNK + n].rearrange("p t n -> p n t"),
                     SILU,
-                    bias=silu_bias[:],
                 )
         for g in range(len(GROUPS)):
             layer2(g)

@@ -30,7 +30,7 @@ GATHER = 256
 JOINT_QUADRANTS = 2
 EARLY = 512
 SCALAR_PLANES = (3, 2)
-GROUPS = ((0, 256), (256, 512), (512, 640), (640, 704), (704, 768))
+GROUPS = ((0, 128), (128, 384), (384, 512), (512, 640), (640, 704), (704, 768))
 V_PIECES = ((0, 256), (256, 384))
 
 
@@ -188,7 +188,7 @@ def tile_picked_sub_mlp_silu_sub_p_kernel(
             w2_bf[:].rearrange("p (m t) -> p m t", t=PACK), w2_raw[:].rearrange("p t m -> p m t")
         )
         nc.vector.quantize_mx(w2_codes[:].bitcast(FP8X4), w2_scales[:], w2_bf[:])
-        for c in (0, 1, 3, 2, 5, 4):
+        for c in range(CHUNKS):
             layer1(1, c)
         for g, (j0, j1) in enumerate(GROUPS):
             for j in range(j0, j1, CHUNK):

@@ -31,6 +31,7 @@ JOINT_QUADRANTS = 2
 EARLY = 512
 SCALAR_PLANES = (3, 2)
 GROUPS = ((0, 128), (128, 384), (384, 512), (512, 640), (640, 704), (704, 768))
+ROWS_AT = (16, 112)
 V_PIECES = ((0, 256), (256, 384))
 
 
@@ -62,9 +63,11 @@ def tile_picked_sub_mlp_silu_sub_p_kernel(
             nc.sync.dma_start(w1_raw[o][:], rows.rearrange("(p j) c -> p j c", j=PACK))
 
         nc.sync.dma_start(offs_sb[:], offs)
-        nc.scalar.dma_start(scales_all[:QUADRANT, :], x_scales.rearrange("o q n -> (o q) n").bitcast(I32))
-        nc.vector.memset(scales_all[QUADRANT : 2 * QUADRANT, :], 0)
-        nc.vector.memset(scales_all[2 * QUADRANT :, :], 0)
+        for o in range(PASSES):
+            nc.scalar.dma_start(scales_all[ROWS_AT[o] : ROWS_AT[o] + 16, :], x_scales[o].bitcast(I32))
+        nc.vector.memset(scales_all[:16, :], 0)
+        nc.vector.memset(scales_all[32:64, :], 0)
+        nc.vector.memset(scales_all[64:112, :], 0)
         load_w1(0, "raw0")
         nc.sync.dma_start(pos_sb[0][:], pos1)
         nc.sync.dma_start(pos_sb[1][:], pos2)
@@ -77,9 +80,9 @@ def tile_picked_sub_mlp_silu_sub_p_kernel(
             planes[o] = keep.tile([P, S], U8, name=f"planes{o}", tag=tag, align_bytes=64)
             nc.vector.memset(planes[o][:].bitcast(I32), 0)
             for q in range(QUADRANTS):
-                src = (o * QUADRANTS + q) * SCALE_ROWS
+                src = ROWS_AT[o] + q * SCALE_ROWS
                 dst = QUADRANT * q + SCALE_ROWS * o
-                queue = nc.scalar if o == 0 and q % 2 else nc.sync
+                queue = nc.scalar if o == 1 or q % 2 else nc.sync
                 queue.dma_start(
                     planes[o][dst : dst + SCALE_ROWS, :].bitcast(I32),
                     scales_picked[src : src + SCALE_ROWS, :].bitcast(I32),

@@ -32,6 +32,7 @@ EARLY = 512
 SCALAR_PLANES = (3, 2)
 GROUPS = ((0, 128), (128, 384), (384, 512), (512, 640), (640, 704), (704, 768))
 ROWS_AT = (16, 112)
+VECTOR_EXTRA = 16
 V_PIECES = ((0, 256), (256, 384))
 
 
@@ -82,7 +83,7 @@ def tile_picked_sub_mlp_silu_sub_p_kernel(
             for q in range(QUADRANTS):
                 src = ROWS_AT[o] + q * SCALE_ROWS
                 dst = QUADRANT * q + SCALE_ROWS * o
-                queue = nc.scalar if o == 1 or q % 2 else nc.sync
+                queue = nc.scalar if o == 0 and q % 2 else nc.sync
                 queue.dma_start(
                     planes[o][dst : dst + SCALE_ROWS, :].bitcast(I32),
                     scales_picked[src : src + SCALE_ROWS, :].bitcast(I32),
@@ -122,7 +123,8 @@ def tile_picked_sub_mlp_silu_sub_p_kernel(
             src = w1_raw[o][:].rearrange("p j (a u r v) -> p u a j r v", u=2, r=2, v=2)
             dst = [w1_bf[o, u][:].rearrange("p (v a r j) -> p a j r v", v=2, r=2, j=PACK) for u in range(2)]
             nc.vector.tensor_copy(dst[0], src[:, 0])
-            nc.scalar.copy(dst[1], src[:, 1])
+            nc.vector.tensor_copy(dst[1][:, :VECTOR_EXTRA], src[:, 1, :VECTOR_EXTRA])
+            nc.scalar.copy(dst[1][:, VECTOR_EXTRA:], src[:, 1, VECTOR_EXTRA:])
 
         def quantize_w1(o, tag):
             w1_codes[o] = keep.tile([P, H], U32, name=f"w1_codes{o}", tag=tag, align_bytes=64)

@@ -75,6 +75,7 @@ def tile_picked_sub_mlp_silu_sub_p_kernel(
         nc.vector.memset(zero[:], 0.0)
         nc.scalar.activation(silu_bias[:], zero[:], SILU)
         load_words(0, "words0")
+        load_w1(1, "raw1")
         nc.vector.tensor_copy(scales_picked[:], scales_all[:].bitcast(U8).indirect(offs_sb[:]))
 
         def move_scales(o, tag):
@@ -83,14 +84,13 @@ def tile_picked_sub_mlp_silu_sub_p_kernel(
             for q in range(QUADRANTS):
                 src = ROWS_AT[o] + q * SCALE_ROWS
                 dst = QUADRANT * q + SCALE_ROWS * o
-                queue = nc.scalar if o == 0 and q % 2 else nc.sync
+                queue = nc.scalar if o == 0 else nc.sync
                 queue.dma_start(
                     planes[o][dst : dst + SCALE_ROWS, :].bitcast(I32),
                     scales_picked[src : src + SCALE_ROWS, :].bitcast(I32),
                 )
 
         move_scales(0, "planes0")
-        load_w1(1, "scales")
 
         x_codes = {}
         w1_bf = {
@@ -179,7 +179,7 @@ def tile_picked_sub_mlp_silu_sub_p_kernel(
             layer1(0, c)
         cast_w1(1)
         quantize_w1(1, "codes1")
-        w2_raw = keep.tile([P, PACK, N], F32, name="w2_raw", tag="scales", align_bytes=64)
+        w2_raw = keep.tile([P, PACK, N], F32, name="w2_raw", tag="raw1", align_bytes=64)
         for u in range(2):
             nc.sync.dma_start(
                 w2_raw[:, 2 * u : 2 * u + 2, :].rearrange("p v m -> p (v m)"),

@@ -70,8 +70,6 @@ def tile_picked_sub_mlp_silu_sub_p_kernel(
         nc.vector.memset(scales_all[32:64, :], 0)
         nc.vector.memset(scales_all[64:112, :], 0)
         load_w1(0, "raw0")
-        nc.sync.dma_start(pos_sb[0][:], pos1)
-        nc.sync.dma_start(pos_sb[1][:], pos2)
         nc.vector.memset(zero[:], 0.0)
         nc.scalar.activation(silu_bias[:], zero[:], SILU)
         load_words(0, "words0")
@@ -188,6 +186,8 @@ def tile_picked_sub_mlp_silu_sub_p_kernel(
         gather_words(1, 0, S, "xc1")
         gate_sb = keep.tile([P, D, V], F32, name="gate_sb", tag="bf11", align_bytes=64)
         nc.sync.dma_start(gate_sb[:], gate.rearrange("d m v -> m d v"))
+        nc.sync.dma_start(pos_sb[0][:], pos1)
+        nc.sync.dma_start(pos_sb[1][:], pos2)
         w2_bf = keep.tile([P, N * PACK], BF16, name="w2_bf", tag="raw0", align_bytes=64)
         nc.vector.tensor_copy(
             w2_bf[:].rearrange("p (m t) -> p m t", t=PACK), w2_raw[:].rearrange("p t m -> p m t")

@@ -31,7 +31,7 @@ JOINT_QUADRANTS = 2
 EARLY = 512
 SCALAR_PLANES = (3, 2)
 GROUPS = ((0, 128), (128, 384), (384, 512), (512, 640), (640, 704), (704, 768))
-ROWS_AT = (16, 112)
+ROWS_AT = (96, 112)
 VECTOR_EXTRA = 16
 V_PIECES = ((0, 256), (256, 384))
 
@@ -63,17 +63,13 @@ def tile_picked_sub_mlp_silu_sub_p_kernel(
             rows = w1[o * K_PASS : (o + 1) * K_PASS, :]
             nc.sync.dma_start(w1_raw[o][:], rows.rearrange("(p j) c -> p j c", j=PACK))
 
+        nc.sync.dma_start(scales_all[96:, :], x_scales.rearrange("o q c -> (o q) c").bitcast(I32))
         nc.sync.dma_start(offs_sb[:], offs)
-        for o in range(PASSES):
-            nc.scalar.dma_start(scales_all[ROWS_AT[o] : ROWS_AT[o] + 16, :], x_scales[o].bitcast(I32))
-        nc.vector.memset(scales_all[:16, :], 0)
-        nc.vector.memset(scales_all[32:64, :], 0)
-        nc.vector.memset(scales_all[64:112, :], 0)
+        nc.vector.memset(scales_all[:96, :], 0)
         load_w1(0, "raw0")
         nc.vector.memset(zero[:], 0.0)
         nc.scalar.activation(silu_bias[:], zero[:], SILU)
         load_words(0, "words0")
-        load_w1(1, "raw1")
         nc.vector.tensor_copy(scales_picked[:], scales_all[:].bitcast(U8).indirect(offs_sb[:]))
 
         def move_scales(o, tag):
@@ -82,13 +78,13 @@ def tile_picked_sub_mlp_silu_sub_p_kernel(
             for q in range(QUADRANTS):
                 src = ROWS_AT[o] + q * SCALE_ROWS
                 dst = QUADRANT * q + SCALE_ROWS * o
-                queue = nc.scalar if o == 0 else nc.sync
-                queue.dma_start(
+                nc.sync.dma_start(
                     planes[o][dst : dst + SCALE_ROWS, :].bitcast(I32),
                     scales_picked[src : src + SCALE_ROWS, :].bitcast(I32),
                 )
 
         move_scales(0, "planes0")
+        load_w1(1, "scales")
 
         x_codes = {}
         w1_bf = {
@@ -124,23 +120,24 @@ def tile_picked_sub_mlp_silu_sub_p_kernel(
             nc.vector.tensor_copy(dst[1][:, :VECTOR_EXTRA], src[:, 1, :VECTOR_EXTRA])
             nc.scalar.copy(dst[1][:, VECTOR_EXTRA:], src[:, 1, VECTOR_EXTRA:])
 
-        def quantize_w1(o, tag):
-            w1_codes[o] = keep.tile([P, H], U32, name=f"w1_codes{o}", tag=tag, align_bytes=64)
-            for t in range(PACK):
-                plane = slice(t * P, (t + 1) * P)
+        def quantize_w1(o, u, tag):
+            codes = keep.tile([P, 2 * P], U32, name=f"w1_codes{o}{u}", tag=tag, align_bytes=64)
+            for e in range(2):
+                t = 2 * u + e
+                w1_codes[o, t] = codes[:, e * P : (e + 1) * P]
                 nc.vector.quantize_mx(
-                    w1_codes[o][:, plane].bitcast(FP8X4),
-                    w1_scales[o][:, plane],
-                    w1_bf[o, t // 2][:, t % 2 * P * PACK : (t % 2 + 1) * P * PACK],
+                    w1_codes[o, t].bitcast(FP8X4),
+                    w1_scales[o][:, t * P : (t + 1) * P],
+                    w1_bf[o, u][:, e * P * PACK : (e + 1) * P * PACK],
                 )
 
-        def layer1(o, c):
+        def layer1(o, c, ts):
             nodes = slice(c * CHUNK, (c + 1) * CHUNK)
-            for t in range(PACK):
+            for t in ts:
                 plane = slice(t * P, (t + 1) * P)
                 nc.tensor.matmul_mx(
                     pre[c][:, t, :],
-                    lhsT=w1_codes[o][:, plane].bitcast(FP8X4),
+                    lhsT=w1_codes[o, t].bitcast(FP8X4),
                     lhsT_scale=w1_scales[o][:, plane],
                     rhs=x_codes[o, c].bitcast(FP8X4),
                     rhs_scale=planes[o][SCALE_ROWS * o :, nodes],
@@ -170,14 +167,18 @@ def tile_picked_sub_mlp_silu_sub_p_kernel(
 
         cast_w1(0)
         load_words(1, "raw0")
-        quantize_w1(0, "codes0")
-        move_scales(1, "bf01")
+        quantize_w1(0, 0, "codes00")
+        move_scales(1, "bf00")
         gather_words(0, 0, S, "xc0")
         for c in range(CHUNKS):
-            layer1(0, c)
+            layer1(0, c, (0, 1))
         cast_w1(1)
-        quantize_w1(1, "codes1")
-        w2_raw = keep.tile([P, PACK, N], F32, name="w2_raw", tag="raw1", align_bytes=64)
+        quantize_w1(0, 1, "scales")
+        for c in range(CHUNKS):
+            layer1(0, c, (2, 3))
+        quantize_w1(1, 0, "codes10")
+        quantize_w1(1, 1, "codes11")
+        w2_raw = keep.tile([P, PACK, N], F32, name="w2_raw", tag="words0", align_bytes=64)
         for u in range(2):
             nc.sync.dma_start(
                 w2_raw[:, 2 * u : 2 * u + 2, :].rearrange("p v m -> p (v m)"),
@@ -194,7 +195,7 @@ def tile_picked_sub_mlp_silu_sub_p_kernel(
         )
         nc.vector.quantize_mx(w2_codes[:].bitcast(FP8X4), w2_scales[:], w2_bf[:])
         for c in range(CHUNKS):
-            layer1(1, c)
+            layer1(1, c, range(PACK))
         for g, (j0, j1) in enumerate(GROUPS):
             for j in range(j0, j1, CHUNK):
                 n = min(CHUNK, j1 - j)

@@ -14,25 +14,27 @@ U8 = mybir.dt.uint8
 FP8X4 = mybir.dt.float8_e4m3fn_x4
 MULT = mybir.AluOpType.mult
 SILU = mybir.ActivationFunctionType.Silu
+IDENTITY = mybir.ActivationFunctionType.Identity
 
 P = 128
 PACK = 4
+PAIR = 2
 K_PASS = P * PACK
 PASSES = K // K_PASS
 QUADRANT = 32
 QUADRANTS = P // QUADRANT
 SCALE_ROWS = 4
+PASS_ROWS = QUADRANTS * SCALE_ROWS
+FIRST_ROW = P - PASSES * PASS_ROWS
 STRIPE = 16
 RUN = 4
+BANKS = 8
 CHUNK = 128
 CHUNKS = S // CHUNK
 GATHER = 256
-JOINT_QUADRANTS = 2
-EARLY = 512
-SCALAR_PLANES = (3, 2)
-GROUPS = ((0, 128), (128, 384), (384, 512), (512, 640), (640, 704), (704, 768))
-ROWS_AT = (96, 112)
 VECTOR_EXTRA = 16
+GROUPS = ((0, 128), (128, 384), (384, 512), (512, 640), (640, 704), (704, 768))
+Y_BANKS = ((0, 1), (2, 3), (4,), (5,))
 V_PIECES = ((0, 256), (256, 384))
 
 
@@ -48,11 +50,11 @@ def tile_picked_sub_mlp_silu_sub_p_kernel(
         pos_sb = [keep.tile([P, V // STRIPE], U16, name=f"pos_sb{d}") for d in range(D)]
         words_all = {}
         scales_picked = keep.tile([P, S], U8, name="scales_picked", align_bytes=64)
-        planes = {}
+        x_scale = {}
         scales_all = keep.tile([P, T // PACK], I32, name="scales_all", tag="scales", align_bytes=64)
         w1_raw = {}
         zero = keep.tile([P, 1], F32, name="zero")
-        silu_bias = keep.tile([P, 1], F32, name="silu_bias")
+        silu_zero = keep.tile([P, 1], F32, name="silu_zero")
 
         def load_words(o, tag):
             words_all[o] = keep.tile([P, T], I32, name=f"words_all{o}", tag=tag, align_bytes=64)
@@ -63,94 +65,103 @@ def tile_picked_sub_mlp_silu_sub_p_kernel(
             rows = w1[o * K_PASS : (o + 1) * K_PASS, :]
             nc.sync.dma_start(w1_raw[o][:], rows.rearrange("(p j) c -> p j c", j=PACK))
 
-        nc.sync.dma_start(scales_all[96:, :], x_scales.rearrange("o q c -> (o q) c").bitcast(I32))
-        nc.sync.dma_start(offs_sb[:], offs)
-        nc.vector.memset(scales_all[:96, :], 0)
-        load_w1(0, "raw0")
-        nc.vector.memset(zero[:], 0.0)
-        nc.scalar.activation(silu_bias[:], zero[:], SILU)
-        load_words(0, "words0")
-        nc.vector.tensor_copy(scales_picked[:], scales_all[:].bitcast(U8).indirect(offs_sb[:]))
-
         def move_scales(o, tag):
-            planes[o] = keep.tile([P, S], U8, name=f"planes{o}", tag=tag, align_bytes=64)
-            nc.vector.memset(planes[o][:].bitcast(I32), 0)
+            x_scale[o] = keep.tile([P, S], U8, name=f"x_scale{o}", tag=tag, align_bytes=64)
+            nc.vector.memset(x_scale[o][:].bitcast(I32), 0)
             for q in range(QUADRANTS):
-                src = ROWS_AT[o] + q * SCALE_ROWS
+                src = FIRST_ROW + o * PASS_ROWS + q * SCALE_ROWS
                 dst = QUADRANT * q + SCALE_ROWS * o
                 nc.sync.dma_start(
-                    planes[o][dst : dst + SCALE_ROWS, :].bitcast(I32),
+                    x_scale[o][dst : dst + SCALE_ROWS, :].bitcast(I32),
                     scales_picked[src : src + SCALE_ROWS, :].bitcast(I32),
                 )
 
-        move_scales(0, "planes0")
+        nc.sync.dma_start(scales_all[FIRST_ROW:, :], x_scales.rearrange("o q c -> (o q) c").bitcast(I32))
+        nc.sync.dma_start(offs_sb[:], offs)
+        nc.vector.memset(scales_all[:FIRST_ROW, :], 0)
+        load_w1(0, "raw0")
+        nc.vector.memset(zero[:], 0.0)
+        nc.scalar.activation(silu_zero[:], zero[:], SILU)
+        load_words(0, "words0")
+        nc.vector.tensor_copy(scales_picked[:], scales_all[:].bitcast(U8).indirect(offs_sb[:]))
+        move_scales(0, "x_scale0")
         load_w1(1, "scales")
 
         x_codes = {}
         w1_bf = {
-            (o, u): keep.tile([P, H * PACK // 2], BF16, name=f"w1_bf{o}{u}", tag=f"bf{o}{u}", align_bytes=64)
+            (o, u): keep.tile([P, PAIR * P * PACK], BF16, name=f"w1_bf{o}{u}", tag=f"bf{o}{u}", align_bytes=64)
             for o in range(PASSES)
-            for u in range(2)
+            for u in range(PAIR)
         }
         w1_codes = {}
         w1_scales = [keep.tile([P, H], U8, name=f"w1_scales{o}", align_bytes=64) for o in range(PASSES)]
         w2_codes = keep.tile([P, N], U32, name="w2_codes", align_bytes=64)
         w2_scales = keep.tile([P, N], U8, name="w2_scales", align_bytes=64)
-        pre = [psum.tile([P, PACK, CHUNK], F32, name=f"pre{c}", tag=f"bank{c}") for c in range(CHUNKS)]
+        pre = {c: psum.tile([P, PACK, CHUNK], F32, name=f"pre{c}", tag=f"bank{c}") for c in range(1, CHUNKS)}
+        head = [
+            psum.tile([P, PAIR, CHUNK], F32, name=f"head{u}", tag=f"bank{(BANKS - 1) * u}") for u in range(PAIR)
+        ]
+        h_pairs = keep.tile([P, PAIR, CHUNK * PAIR], BF16, name="h_pairs", align_bytes=64)
         widths = [j1 - j0 for j0, j1 in GROUPS]
         h_bf = [keep.tile([P, n * PACK], BF16, name=f"h_bf{g}", align_bytes=64) for g, n in enumerate(widths)]
-        h_codes = [keep.tile([P, n], U32, name=f"h_codes{g}", align_bytes=64) for g, n in enumerate(widths)]
+        h_codes = {}
         h_scales = [keep.tile([P, n], U8, name=f"h_scales{g}", align_bytes=64) for g, n in enumerate(widths)]
         y_sb = keep.tile([P, S], F32, name="y_sb")
+        y_ps = {}
 
-        def gather_words(o, j0, j1, tag):
-            codes = keep.tile([P, j1 - j0], U32, name=f"x_codes{o}_{j0}", tag=tag, align_bytes=64)
-            for j in range(j0, j1, GATHER):
+        def gather_words(o):
+            codes = keep.tile([P, S], U32, name=f"x_codes{o}", align_bytes=64)
+            for j in range(0, S, GATHER):
                 entries = offs_sb[:, j // STRIPE : (j + GATHER) // STRIPE]
-                nc.vector.tensor_copy(
-                    codes[:, j - j0 : j - j0 + GATHER], words_all[o][:].bitcast(U32).indirect(entries)
-                )
-            for j in range(j0, j1, CHUNK):
-                x_codes[o, j // CHUNK] = codes[:, j - j0 : j - j0 + CHUNK]
+                nc.vector.tensor_copy(codes[:, j : j + GATHER], words_all[o][:].bitcast(U32).indirect(entries))
+            for c in range(CHUNKS):
+                x_codes[o, c] = codes[:, c * CHUNK : (c + 1) * CHUNK]
 
         def cast_w1(o):
-            src = w1_raw[o][:].rearrange("p j (a u r v) -> p u a j r v", u=2, r=2, v=2)
-            dst = [w1_bf[o, u][:].rearrange("p (v a r j) -> p a j r v", v=2, r=2, j=PACK) for u in range(2)]
+            src = w1_raw[o][:].rearrange("p j (a u r v) -> p u a j r v", u=PAIR, r=2, v=PAIR)
+            dst = [
+                w1_bf[o, u][:].rearrange("p (v a r j) -> p a j r v", v=PAIR, r=2, j=PACK) for u in range(PAIR)
+            ]
             nc.vector.tensor_copy(dst[0], src[:, 0])
             nc.vector.tensor_copy(dst[1][:, :VECTOR_EXTRA], src[:, 1, :VECTOR_EXTRA])
             nc.scalar.copy(dst[1][:, VECTOR_EXTRA:], src[:, 1, VECTOR_EXTRA:])
 
         def quantize_w1(o, u, tag):
-            codes = keep.tile([P, 2 * P], U32, name=f"w1_codes{o}{u}", tag=tag, align_bytes=64)
-            for e in range(2):
-                t = 2 * u + e
-                w1_codes[o, t] = codes[:, e * P : (e + 1) * P]
+            codes = keep.tile([P, PAIR * P], U32, name=f"w1_codes{o}{u}", tag=tag, align_bytes=64)
+            for v in range(PAIR):
+                t = PAIR * u + v
+                w1_codes[o, t] = codes[:, v * P : (v + 1) * P]
                 nc.vector.quantize_mx(
                     w1_codes[o, t].bitcast(FP8X4),
                     w1_scales[o][:, t * P : (t + 1) * P],
-                    w1_bf[o, u][:, e * P * PACK : (e + 1) * P * PACK],
+                    w1_bf[o, u][:, v * P * PACK : (v + 1) * P * PACK],
                 )
 
-        def layer1(o, c, ts):
-            nodes = slice(c * CHUNK, (c + 1) * CHUNK)
-            for t in ts:
-                plane = slice(t * P, (t + 1) * P)
+        def layer1(o, c, planes):
+            in_bank = PACK if c else PAIR
+            for t in planes:
                 nc.tensor.matmul_mx(
-                    pre[c][:, t, :],
+                    pre[c][:, t, :] if c else head[t // PAIR][:, t % PAIR, :],
                     lhsT=w1_codes[o, t].bitcast(FP8X4),
-                    lhsT_scale=w1_scales[o][:, plane],
+                    lhsT_scale=w1_scales[o][:, t * P : (t + 1) * P],
                     rhs=x_codes[o, c].bitcast(FP8X4),
-                    rhs_scale=planes[o][SCALE_ROWS * o :, nodes],
-                    start=(o == 0 and t == 0),
-                    stop=(o == PASSES - 1 and t == PACK - 1),
+                    rhs_scale=x_scale[o][SCALE_ROWS * o :, c * CHUNK : (c + 1) * CHUNK],
+                    start=(o == 0 and t % in_bank == 0),
+                    stop=(o == PASSES - 1 and (t + 1) % in_bank == 0),
                 )
+
+        def quantize_h(g, tag):
+            h_codes[g] = keep.tile([P, widths[g]], U32, name=f"h_codes{g}", tag=tag, align_bytes=64)
+            nc.vector.quantize_mx(h_codes[g][:].bitcast(FP8X4), h_scales[g][:], h_bf[g][:])
 
         def layer2(g):
             j0, j1 = GROUPS[g]
-            nc.vector.quantize_mx(h_codes[g][:].bitcast(FP8X4), h_scales[g][:], h_bf[g][:])
-            y_ps = psum.tile([P, widths[g]], F32, name=f"y_ps{g}", tag=f"bank{(CHUNKS + g) % 8}")
+            b = [g in members for members in Y_BANKS].index(True)
+            b0, b1 = GROUPS[Y_BANKS[b][0]][0], GROUPS[Y_BANKS[b][-1]][1]
+            if b not in y_ps:
+                y_ps[b] = psum.tile([P, b1 - b0], F32, name=f"y_ps{b}", tag=f"bank{(CHUNKS + b) % BANKS}")
             nc.tensor.matmul_mx(
-                y_ps[:],
+                y_ps[b][:, j0 - b0 : j1 - b0],
                 lhsT=w2_codes[:].bitcast(FP8X4),
                 lhsT_scale=w2_scales[:],
                 rhs=h_codes[g][:].bitcast(FP8X4),
@@ -158,46 +169,55 @@ def tile_picked_sub_mlp_silu_sub_p_kernel(
                 start=True,
                 stop=True,
             )
-            if g == 1:
-                nc.scalar.activation(y_sb[:, j0:j1], y_ps[:], mybir.ActivationFunctionType.Identity, bias=silu_bias[:])
-            elif g > 1:
-                nc.scalar.copy(y_sb[:, j0:j1], y_ps[:])
+            if j1 < b1:
+                return
+            if b == 0:
+                nc.scalar.activation(y_sb[:, b0:b1], y_ps[b][:], IDENTITY, bias=silu_zero[:])
             else:
-                nc.vector.tensor_copy(y_sb[:, j0:j1], y_ps[:])
+                nc.scalar.copy(y_sb[:, b0:b1], y_ps[b][:])
 
         cast_w1(0)
         load_words(1, "raw0")
         quantize_w1(0, 0, "codes00")
         move_scales(1, "bf00")
-        gather_words(0, 0, S, "xc0")
+        gather_words(0)
         for c in range(CHUNKS):
-            layer1(0, c, (0, 1))
+            layer1(0, c, range(PAIR))
         cast_w1(1)
         quantize_w1(0, 1, "scales")
         for c in range(CHUNKS):
-            layer1(0, c, (2, 3))
+            layer1(0, c, range(PAIR, PACK))
         quantize_w1(1, 0, "codes10")
         quantize_w1(1, 1, "codes11")
         w2_raw = keep.tile([P, PACK, N], F32, name="w2_raw", tag="words0", align_bytes=64)
-        for u in range(2):
+        for u in range(PAIR):
             nc.sync.dma_start(
-                w2_raw[:, 2 * u : 2 * u + 2, :].rearrange("p v m -> p (v m)"),
-                w2.rearrange("(a u r v) m -> u a r (v m)", u=2, r=2, v=2)[u],
+                w2_raw[:, PAIR * u : PAIR * (u + 1), :].rearrange("p v m -> p (v m)"),
+                w2.rearrange("(a u r v) m -> u a r (v m)", u=PAIR, r=2, v=PAIR)[u],
             )
-        gather_words(1, 0, S, "xc1")
+        gather_words(1)
         gate_sb = keep.tile([P, D, V], F32, name="gate_sb", tag="bf11", align_bytes=64)
         nc.sync.dma_start(gate_sb[:], gate.rearrange("d m v -> m d v"))
         nc.sync.dma_start(pos_sb[0][:], pos1)
         nc.sync.dma_start(pos_sb[1][:], pos2)
         w2_bf = keep.tile([P, N * PACK], BF16, name="w2_bf", tag="raw0", align_bytes=64)
         nc.vector.tensor_copy(
-            w2_bf[:].rearrange("p (m t) -> p m t", t=PACK), w2_raw[:].rearrange("p t m -> p m t")
+            w2_bf[:].rearrange("p (a m t) -> p a t m", m=RUN, t=PACK),
+            w2_raw[:].rearrange("p t (a m) -> p a t m", m=RUN),
         )
-        nc.vector.quantize_mx(w2_codes[:].bitcast(FP8X4), w2_scales[:], w2_bf[:])
         for c in range(CHUNKS):
             layer1(1, c, range(PACK))
+
+        for u in range(PAIR):
+            nc.scalar.activation(
+                h_pairs[:, u, :].rearrange("p (n v) -> p n v", v=PAIR), head[u][:].rearrange("p v n -> p n v"), SILU
+            )
+        nc.vector.tensor_copy(
+            h_bf[0][:].bitcast(F32).rearrange("p (n u) -> p n u", u=PAIR),
+            h_pairs[:].rearrange("p u w -> p (u w)").bitcast(F32).rearrange("p (u n) -> p n u", u=PAIR),
+        )
         for g, (j0, j1) in enumerate(GROUPS):
-            for j in range(j0, j1, CHUNK):
+            for j in range(max(j0, CHUNK), j1, CHUNK):
                 n = min(CHUNK, j1 - j)
                 h_out = h_bf[g][:, (j - j0) * PACK : (j - j0 + n) * PACK]
                 nc.scalar.activation(
@@ -205,7 +225,11 @@ def tile_picked_sub_mlp_silu_sub_p_kernel(
                     pre[j // CHUNK][:, :, j % CHUNK : j % CHUNK + n].rearrange("p t n -> p n t"),
                     SILU,
                 )
-        for g in range(len(GROUPS)):
+        quantize_h(0, "words0")
+        nc.vector.quantize_mx(w2_codes[:].bitcast(FP8X4), w2_scales[:], w2_bf[:])
+        layer2(0)
+        for g in range(1, len(GROUPS)):
+            quantize_h(g, f"h_codes{g}")
             layer2(g)
 
         first = keep.tile([P, V], F32, name="first")

@@ -34,7 +34,8 @@ CHUNKS = S // CHUNK
 GATHER = 256
 VECTOR_EXTRA = 16
 GROUPS = ((0, 128), (128, 384), (384, 512), (512, 640), (640, 704), (704, 768))
-Y_BANKS = ((0, 1), (2, 3), (4,), (5,))
+HEAD = ((0, 1), (1, 2), (2, 4))
+Y_BANKS = ((0, 1, 2), (3, 4), (5,))
 V_PIECES = ((0, 256), (256, 384))
 
 
@@ -98,10 +99,11 @@ def tile_picked_sub_mlp_silu_sub_p_kernel(
         w2_codes = keep.tile([P, N], U32, name="w2_codes", align_bytes=64)
         w2_scales = keep.tile([P, N], U8, name="w2_scales", align_bytes=64)
         pre = {c: psum.tile([P, PACK, CHUNK], F32, name=f"pre{c}", tag=f"bank{c}") for c in range(1, CHUNKS)}
-        head = [
-            psum.tile([P, PAIR, CHUNK], F32, name=f"head{u}", tag=f"bank{(BANKS - 1) * u}") for u in range(PAIR)
-        ]
-        h_pairs = keep.tile([P, PAIR, CHUNK * PAIR], BF16, name="h_pairs", align_bytes=64)
+        head = {
+            t0: psum.tile([P, t1 - t0, CHUNK], F32, name=f"head{t0}", tag=f"bank{b}")
+            for b, (t0, t1) in zip((0, CHUNKS, CHUNKS + 1), HEAD)
+        }
+        h_planes = keep.tile([P, PACK, CHUNK], BF16, name="h_planes", align_bytes=64)
         widths = [j1 - j0 for j0, j1 in GROUPS]
         h_bf = [keep.tile([P, n * PACK], BF16, name=f"h_bf{g}", align_bytes=64) for g, n in enumerate(widths)]
         h_codes = {}
@@ -138,16 +140,16 @@ def tile_picked_sub_mlp_silu_sub_p_kernel(
                 )
 
         def layer1(o, c, planes):
-            in_bank = PACK if c else PAIR
             for t in planes:
+                t0, t1 = (0, PACK) if c else [span for span in HEAD if t < span[1]][0]
                 nc.tensor.matmul_mx(
-                    pre[c][:, t, :] if c else head[t // PAIR][:, t % PAIR, :],
+                    (pre[c] if c else head[t0])[:, t - t0, :],
                     lhsT=w1_codes[o, t].bitcast(FP8X4),
                     lhsT_scale=w1_scales[o][:, t * P : (t + 1) * P],
                     rhs=x_codes[o, c].bitcast(FP8X4),
                     rhs_scale=x_scale[o][SCALE_ROWS * o :, c * CHUNK : (c + 1) * CHUNK],
-                    start=(o == 0 and t % in_bank == 0),
-                    stop=(o == PASSES - 1 and (t + 1) % in_bank == 0),
+                    start=(o == 0 and t == t0),
+                    stop=(o == PASSES - 1 and t == t1 - 1),
                 )
 
         def quantize_h(g, tag):
@@ -208,13 +210,11 @@ def tile_picked_sub_mlp_silu_sub_p_kernel(
         for c in range(CHUNKS):
             layer1(1, c, range(PACK))
 
-        for u in range(PAIR):
-            nc.scalar.activation(
-                h_pairs[:, u, :].rearrange("p (n v) -> p n v", v=PAIR), head[u][:].rearrange("p v n -> p n v"), SILU
-            )
+        for t0, t1 in HEAD:
+            nc.scalar.activation(h_planes[:, t0:t1, :], head[t0][:], SILU)
         nc.vector.tensor_copy(
-            h_bf[0][:].bitcast(F32).rearrange("p (n u) -> p n u", u=PAIR),
-            h_pairs[:].rearrange("p u w -> p (u w)").bitcast(F32).rearrange("p (u n) -> p n u", u=PAIR),
+            h_bf[0][:].rearrange("p (a m t) -> p a t m", m=RUN, t=PACK),
+            h_planes[:].rearrange("p t (a m) -> p a t m", m=RUN),
         )
         for g, (j0, j1) in enumerate(GROUPS):
             for j in range(max(j0, CHUNK), j1, CHUNK):

@@ -15,6 +15,7 @@ FP8X4 = mybir.dt.float8_e4m3fn_x4
 MULT = mybir.AluOpType.mult
 SILU = mybir.ActivationFunctionType.Silu
 IDENTITY = mybir.ActivationFunctionType.Identity
+COPY = mybir.ActivationFunctionType.Copy
 
 P = 128
 PACK = 4
@@ -31,7 +32,7 @@ RUN = 4
 BANKS = 8
 CHUNK = 128
 CHUNKS = S // CHUNK
-GATHER = 256
+GATHERS = ((256, 256, 256), (128, 128, 256, 256))
 VECTOR_EXTRA = 16
 GROUPS = ((0, 128), (128, 384), (384, 512), (512, 640), (640, 704), (704, 768))
 HEAD = ((0, 1), (1, 2), (2, 4))
@@ -113,9 +114,11 @@ def tile_picked_sub_mlp_silu_sub_p_kernel(
 
         def gather_words(o):
             codes = keep.tile([P, S], U32, name=f"x_codes{o}", align_bytes=64)
-            for j in range(0, S, GATHER):
-                entries = offs_sb[:, j // STRIPE : (j + GATHER) // STRIPE]
-                nc.vector.tensor_copy(codes[:, j : j + GATHER], words_all[o][:].bitcast(U32).indirect(entries))
+            j = 0
+            for n in GATHERS[o]:
+                entries = offs_sb[:, j // STRIPE : (j + n) // STRIPE]
+                nc.vector.tensor_copy(codes[:, j : j + n], words_all[o][:].bitcast(U32).indirect(entries))
+                j = j + n
             for c in range(CHUNKS):
                 x_codes[o, c] = codes[:, c * CHUNK : (c + 1) * CHUNK]
 
@@ -238,7 +241,9 @@ def tile_picked_sub_mlp_silu_sub_p_kernel(
         for i, (v0, v1) in enumerate(V_PIECES):
             term = keep.tile([P, v1 - v0], F32, name=f"second{i}")
             entries = pos_sb[1][:, v0 // STRIPE : v1 // STRIPE]
-            nc.vector.tensor_tensor(term[:], y_sb[:].indirect(entries), gate_sb[:, 1, v0:v1], MULT)
+            fetched = keep.tile([P, v1 - v0], F32, name=f"fetched{i}")
+            nc.scalar.activation(fetched[:], y_sb[:].indirect(entries), COPY)
+            nc.vector.tensor_tensor(term[:], fetched[:], gate_sb[:, 1, v0:v1], MULT)
             second.append(term)
         for i, (v0, v1) in enumerate(V_PIECES):
             res = keep.tile([P, v1 - v0], F32, name=f"res{i}")

@@ -33,7 +33,7 @@ BANKS = 8
 CHUNK = 128
 CHUNKS = S // CHUNK
 GATHERS = ((256, 256, 256), (128, 128, 256, 256))
-VECTOR_EXTRA = 16
+VECTOR_EXTRA = (16, 0)
 GROUPS = ((0, 128), (128, 384), (384, 512), (512, 640), (640, 704), (704, 768))
 HEAD = ((0, 1), (1, 2), (2, 4))
 Y_BANKS = ((0, 1, 2), (3, 4), (5,))
@@ -96,7 +96,13 @@ def tile_picked_sub_mlp_silu_sub_p_kernel(
             for u in range(PAIR)
         }
         w1_codes = {}
-        w1_scales = [keep.tile([P, H], U8, name=f"w1_scales{o}", align_bytes=64) for o in range(PASSES)]
+        w1_scales = {}
+        for o in range(PASSES):
+            for t in range(PACK):
+                if o == 1 and t % PAIR == 0:
+                    w1_scales[o, t] = w1_scales[0, PAIR + t // PAIR][SCALE_ROWS:, :]
+                else:
+                    w1_scales[o, t] = keep.tile([P, P], U8, name=f"w1_scales{o}{t}", align_bytes=64)[:]
         w2_codes = keep.tile([P, N], U32, name="w2_codes", align_bytes=64)
         w2_scales = keep.tile([P, N], U8, name="w2_scales", align_bytes=64)
         pre = {c: psum.tile([P, PACK, CHUNK], F32, name=f"pre{c}", tag=f"bank{c}") for c in range(1, CHUNKS)}
@@ -128,8 +134,10 @@ def tile_picked_sub_mlp_silu_sub_p_kernel(
                 w1_bf[o, u][:].rearrange("p (v a r j) -> p a j r v", v=PAIR, r=2, j=PACK) for u in range(PAIR)
             ]
             nc.vector.tensor_copy(dst[0], src[:, 0])
-            nc.vector.tensor_copy(dst[1][:, :VECTOR_EXTRA], src[:, 1, :VECTOR_EXTRA])
-            nc.scalar.copy(dst[1][:, VECTOR_EXTRA:], src[:, 1, VECTOR_EXTRA:])
+            extra = VECTOR_EXTRA[o]
+            if extra:
+                nc.vector.tensor_copy(dst[1][:, :extra], src[:, 1, :extra])
+            nc.scalar.copy(dst[1][:, extra:], src[:, 1, extra:])
 
         def quantize_w1(o, u, tag):
             codes = keep.tile([P, PAIR * P], U32, name=f"w1_codes{o}{u}", tag=tag, align_bytes=64)
@@ -138,7 +146,7 @@ def tile_picked_sub_mlp_silu_sub_p_kernel(
                 w1_codes[o, t] = codes[:, v * P : (v + 1) * P]
                 nc.vector.quantize_mx(
                     w1_codes[o, t].bitcast(FP8X4),
-                    w1_scales[o][:, t * P : (t + 1) * P],
+                    w1_scales[o, t],
                     w1_bf[o, u][:, v * P * PACK : (v + 1) * P * PACK],
                 )
 
@@ -148,7 +156,7 @@ def tile_picked_sub_mlp_silu_sub_p_kernel(
                 nc.tensor.matmul_mx(
                     (pre[c] if c else head[t0])[:, t - t0, :],
                     lhsT=w1_codes[o, t].bitcast(FP8X4),
-                    lhsT_scale=w1_scales[o][:, t * P : (t + 1) * P],
+                    lhsT_scale=w1_scales[o, t],
                     rhs=x_codes[o, c].bitcast(FP8X4),
                     rhs_scale=x_scale[o][SCALE_ROWS * o :, c * CHUNK : (c + 1) * CHUNK],
                     start=(o == 0 and t == t0),
@@ -184,16 +192,16 @@ def tile_picked_sub_mlp_silu_sub_p_kernel(
         cast_w1(0)
         load_words(1, "raw0")
         quantize_w1(0, 0, "codes00")
+        quantize_w1(0, 1, "codes01")
         move_scales(1, "bf00")
         gather_words(0)
         for c in range(CHUNKS):
             layer1(0, c, range(PAIR))
         cast_w1(1)
-        quantize_w1(0, 1, "scales")
-        for c in range(CHUNKS):
-            layer1(0, c, range(PAIR, PACK))
-        quantize_w1(1, 0, "codes10")
-        quantize_w1(1, 1, "codes11")
+        for u in range(PAIR):
+            quantize_w1(1, u, f"codes1{u}")
+            for c in range(CHUNKS):
+                layer1(0, c, [PAIR + u])
         w2_raw = keep.tile([P, PACK, N], F32, name="w2_raw", tag="words0", align_bytes=64)
         for u in range(PAIR):
             nc.sync.dma_start(

@@ -32,11 +32,12 @@ RUN = 4
 BANKS = 8
 CHUNK = 128
 CHUNKS = S // CHUNK
+WIDEST = 256
 GATHERS = ((256, 256, 256), (128, 128, 256, 256))
 VECTOR_EXTRA = (16, 0)
-GROUPS = ((0, 128), (128, 384), (384, 512), (512, 640), (640, 704), (704, 768))
+GROUPS = ((0, 256), (256, 512), (512, 640), (640, 704), (704, 768))
 HEAD = ((0, 1), (1, 2), (2, 4))
-Y_BANKS = ((0, 1, 2), (3, 4), (5,))
+Y_BANKS = ((0, 1), (2, 3), (4,))
 V_PIECES = ((0, 256), (256, 384))
 
 
@@ -96,13 +97,13 @@ def tile_picked_sub_mlp_silu_sub_p_kernel(
             for u in range(PAIR)
         }
         w1_codes = {}
+        scale_tiles = [keep.tile([P, PAIR * P], U8, name=f"w1_scales{i}", align_bytes=64) for i in range(3)]
         w1_scales = {}
-        for o in range(PASSES):
-            for t in range(PACK):
-                if o == 1 and t % PAIR == 0:
-                    w1_scales[o, t] = w1_scales[0, PAIR + t // PAIR][SCALE_ROWS:, :]
-                else:
-                    w1_scales[o, t] = keep.tile([P, P], U8, name=f"w1_scales{o}{t}", align_bytes=64)[:]
+        for v in range(PAIR):
+            w1_scales[0, v] = scale_tiles[0][:, v * P : (v + 1) * P]
+            w1_scales[0, PAIR + v] = scale_tiles[1 + v][:, :P]
+            for u in range(PAIR):
+                w1_scales[1, PAIR * u + v] = scale_tiles[1 + u][SCALE_ROWS:, v * P : (v + 1) * P]
         w2_codes = keep.tile([P, N], U32, name="w2_codes", align_bytes=64)
         w2_scales = keep.tile([P, N], U8, name="w2_scales", align_bytes=64)
         pre = {c: psum.tile([P, PACK, CHUNK], F32, name=f"pre{c}", tag=f"bank{c}") for c in range(1, CHUNKS)}
@@ -142,13 +143,14 @@ def tile_picked_sub_mlp_silu_sub_p_kernel(
         def quantize_w1(o, u, tag):
             codes = keep.tile([P, PAIR * P], U32, name=f"w1_codes{o}{u}", tag=tag, align_bytes=64)
             for v in range(PAIR):
-                t = PAIR * u + v
-                w1_codes[o, t] = codes[:, v * P : (v + 1) * P]
-                nc.vector.quantize_mx(
-                    w1_codes[o, t].bitcast(FP8X4),
-                    w1_scales[o, t],
-                    w1_bf[o, u][:, v * P * PACK : (v + 1) * P * PACK],
-                )
+                w1_codes[o, PAIR * u + v] = codes[:, v * P : (v + 1) * P]
+            if (o, u) != (0, 1):
+                scales = scale_tiles[o + u][SCALE_ROWS * o :, :]
+                nc.vector.quantize_mx(codes[:].bitcast(FP8X4), scales, w1_bf[o, u][:])
+                return
+            for v in range(PAIR):
+                values = w1_bf[o, u][:, v * P * PACK : (v + 1) * P * PACK]
+                nc.vector.quantize_mx(w1_codes[o, PAIR + v].bitcast(FP8X4), w1_scales[o, PAIR + v], values)
 
         def layer1(o, c, planes):
             for t in planes:
@@ -173,15 +175,17 @@ def tile_picked_sub_mlp_silu_sub_p_kernel(
             b0, b1 = GROUPS[Y_BANKS[b][0]][0], GROUPS[Y_BANKS[b][-1]][1]
             if b not in y_ps:
                 y_ps[b] = psum.tile([P, b1 - b0], F32, name=f"y_ps{b}", tag=f"bank{(CHUNKS + b) % BANKS}")
-            nc.tensor.matmul_mx(
-                y_ps[b][:, j0 - b0 : j1 - b0],
-                lhsT=w2_codes[:].bitcast(FP8X4),
-                lhsT_scale=w2_scales[:],
-                rhs=h_codes[g][:].bitcast(FP8X4),
-                rhs_scale=h_scales[g][:],
-                start=True,
-                stop=True,
-            )
+            for j in range(j0, j1, WIDEST):
+                n = min(WIDEST, j1 - j)
+                nc.tensor.matmul_mx(
+                    y_ps[b][:, j - b0 : j - b0 + n],
+                    lhsT=w2_codes[:].bitcast(FP8X4),
+                    lhsT_scale=w2_scales[:],
+                    rhs=h_codes[g][:, j - j0 : j - j0 + n].bitcast(FP8X4),
+                    rhs_scale=h_scales[g][:, j - j0 : j - j0 + n],
+                    start=True,
+                    stop=True,
+                )
             if j1 < b1:
                 return
             if b == 0:
@@ -224,7 +228,7 @@ def tile_picked_sub_mlp_silu_sub_p_kernel(
         for t0, t1 in HEAD:
             nc.scalar.activation(h_planes[:, t0:t1, :], head[t0][:], SILU)
         nc.vector.tensor_copy(
-            h_bf[0][:].rearrange("p (a m t) -> p a t m", m=RUN, t=PACK),
+            h_bf[0][:, : CHUNK * PACK].rearrange("p (a m t) -> p a t m", m=RUN, t=PACK),
             h_planes[:].rearrange("p t (a m) -> p a t m", m=RUN),
         )
         for g, (j0, j1) in enumerate(GROUPS):
@@ -236,10 +240,8 @@ def tile_picked_sub_mlp_silu_sub_p_kernel(
                     pre[j // CHUNK][:, :, j % CHUNK : j % CHUNK + n].rearrange("p t n -> p n t"),
                     SILU,
                 )
-        quantize_h(0, "words0")
         nc.vector.quantize_mx(w2_codes[:].bitcast(FP8X4), w2_scales[:], w2_bf[:])
-        layer2(0)
-        for g in range(1, len(GROUPS)):
+        for g in range(len(GROUPS)):
             quantize_h(g, f"h_codes{g}")
             layer2(g)
 

@@ -27,6 +27,7 @@ QUADRANTS = P // QUADRANT
 SCALE_ROWS = 4
 PASS_ROWS = QUADRANTS * SCALE_ROWS
 FIRST_ROW = P - PASSES * PASS_ROWS
+X_ROW = (12, 4)
 STRIPE = 16
 RUN = 4
 BANKS = 8
@@ -70,14 +71,17 @@ def tile_picked_sub_mlp_silu_sub_p_kernel(
 
         def move_scales(o, tag):
             x_scale[o] = keep.tile([P, S], U8, name=f"x_scale{o}", tag=tag, align_bytes=64)
-            nc.vector.memset(x_scale[o][:].bitcast(I32), 0)
-            for q in range(QUADRANTS):
-                src = FIRST_ROW + o * PASS_ROWS + q * SCALE_ROWS
-                dst = QUADRANT * q + SCALE_ROWS * o
+            rows = [(FIRST_ROW + o * PASS_ROWS + q * SCALE_ROWS, QUADRANT * q + X_ROW[o]) for q in range(QUADRANTS)]
+            in_place = rows[-1][0] == rows[-1][1]
+            zeroed = FIRST_ROW if in_place else P
+            nc.vector.memset(x_scale[o][:zeroed, :].bitcast(I32), 0)
+            for src, dst in rows[: zeroed // QUADRANT]:
                 nc.sync.dma_start(
                     x_scale[o][dst : dst + SCALE_ROWS, :].bitcast(I32),
                     scales_picked[src : src + SCALE_ROWS, :].bitcast(I32),
                 )
+            if in_place:
+                nc.vector.tensor_copy(x_scale[o][zeroed:, :].bitcast(I32), scales_picked[zeroed:, :].bitcast(I32))
 
         nc.sync.dma_start(scales_all[FIRST_ROW:, :], x_scales.rearrange("o q c -> (o q) c").bitcast(I32))
         nc.sync.dma_start(offs_sb[:], offs)
@@ -160,7 +164,7 @@ def tile_picked_sub_mlp_silu_sub_p_kernel(
                     lhsT=w1_codes[o, t].bitcast(FP8X4),
                     lhsT_scale=w1_scales[o, t],
                     rhs=x_codes[o, c].bitcast(FP8X4),
-                    rhs_scale=x_scale[o][SCALE_ROWS * o :, c * CHUNK : (c + 1) * CHUNK],
+                    rhs_scale=x_scale[o][X_ROW[o] :, c * CHUNK : (c + 1) * CHUNK],
                     start=(o == 0 and t == t0),
                     stop=(o == PASSES - 1 and t == t1 - 1),
                 )

@@ -39,7 +39,7 @@ VECTOR_EXTRA = (16, 0)
 GROUPS = ((0, 256), (256, 512), (512, 640), (640, 704), (704, 768))
 HEAD = ((0, 1), (1, 2), (2, 4))
 Y_BANKS = ((0, 1), (2, 3), (4,))
-V_PIECES = ((0, 256), (256, 384))
+V_PIECES = ((0, 128), (128, 384))
 
 
 def tile_picked_sub_mlp_silu_sub_p_kernel(
@@ -249,17 +249,16 @@ def tile_picked_sub_mlp_silu_sub_p_kernel(
             quantize_h(g, f"h_codes{g}")
             layer2(g)
 
+        (a0, a1), (b0, b1) = V_PIECES
         first = keep.tile([P, V], F32, name="first")
+        second = keep.tile([P, V], F32, name="second")
+        fetched = keep.tile([P, b1 - b0], F32, name="fetched")
+        nc.scalar.activation(fetched[:], y_sb[:].indirect(pos_sb[1][:, b0 // STRIPE : b1 // STRIPE]), COPY)
         nc.vector.tensor_tensor(first[:], y_sb[:].indirect(pos_sb[0][:]), gate_sb[:, 0, :], MULT)
-        second = []
-        for i, (v0, v1) in enumerate(V_PIECES):
-            term = keep.tile([P, v1 - v0], F32, name=f"second{i}")
-            entries = pos_sb[1][:, v0 // STRIPE : v1 // STRIPE]
-            fetched = keep.tile([P, v1 - v0], F32, name=f"fetched{i}")
-            nc.scalar.activation(fetched[:], y_sb[:].indirect(entries), COPY)
-            nc.vector.tensor_tensor(term[:], fetched[:], gate_sb[:, 1, v0:v1], MULT)
-            second.append(term)
+        entries = pos_sb[1][:, a0 // STRIPE : a1 // STRIPE]
+        nc.vector.tensor_tensor(second[:, a0:a1], y_sb[:].indirect(entries), gate_sb[:, 1, a0:a1], MULT)
+        nc.vector.tensor_tensor(second[:, b0:b1], fetched[:], gate_sb[:, 1, b0:b1], MULT)
         for i, (v0, v1) in enumerate(V_PIECES):
             res = keep.tile([P, v1 - v0], F32, name=f"res{i}")
-            nc.vector.tensor_add(res[:], first[:, v0:v1], second[i][:])
+            nc.vector.tensor_add(res[:], first[:, v0:v1], second[:, v0:v1])
             nc.sync.dma_start(out[:, v0:v1], res[:])

@@ -39,7 +39,8 @@ VECTOR_EXTRA = (16, 0)
 GROUPS = ((0, 256), (256, 512), (512, 640), (640, 704), (704, 768))
 HEAD = ((0, 1), (1, 2), (2, 4))
 Y_BANKS = ((0, 1), (2, 3), (4,))
-V_PIECES = ((0, 128), (128, 384))
+OWN = 128
+V_PIECES = ((0, 128), (128, 256), (256, 384))
 
 
 def tile_picked_sub_mlp_silu_sub_p_kernel(
@@ -249,7 +250,7 @@ def tile_picked_sub_mlp_silu_sub_p_kernel(
             quantize_h(g, f"h_codes{g}")
             layer2(g)
 
-        (a0, a1), (b0, b1) = V_PIECES
+        a0, a1, b0, b1 = 0, OWN, OWN, V
         first = keep.tile([P, V], F32, name="first")
         second = keep.tile([P, V], F32, name="second")
         fetched = keep.tile([P, b1 - b0], F32, name="fetched")

@@ -18,6 +18,7 @@ IDENTITY = mybir.ActivationFunctionType.Identity
 COPY = mybir.ActivationFunctionType.Copy
 
 P = 128
+ALIGN = 256
 PACK = 4
 PAIR = 2
 K_PASS = P * PACK
@@ -54,24 +55,24 @@ def tile_picked_sub_mlp_silu_sub_p_kernel(
         offs_sb = keep.tile([P, S // STRIPE], U16, name="offs_sb")
         pos_sb = [keep.tile([P, V // STRIPE], U16, name=f"pos_sb{d}") for d in range(D)]
         words_all = {}
-        scales_picked = keep.tile([P, S], U8, name="scales_picked", align_bytes=64)
+        scales_picked = keep.tile([P, S], U8, name="scales_picked", align_bytes=ALIGN)
         x_scale = {}
-        scales_all = keep.tile([P, T // PACK], I32, name="scales_all", tag="scales", align_bytes=64)
+        scales_all = keep.tile([P, T // PACK], I32, name="scales_all", tag="scales", align_bytes=ALIGN)
         w1_raw = {}
         zero = keep.tile([P, 1], F32, name="zero")
         silu_zero = keep.tile([P, 1], F32, name="silu_zero")
 
         def load_words(o, tag):
-            words_all[o] = keep.tile([P, T], I32, name=f"words_all{o}", tag=tag, align_bytes=64)
+            words_all[o] = keep.tile([P, T], I32, name=f"words_all{o}", tag=tag, align_bytes=ALIGN)
             nc.sync.dma_start(words_all[o][:], x_words[o].rearrange("p n t -> p (n t)").bitcast(I32))
 
         def load_w1(o, tag):
-            w1_raw[o] = keep.tile([P, PACK, H], F32, name=f"w1_raw{o}", tag=tag, align_bytes=64)
+            w1_raw[o] = keep.tile([P, PACK, H], F32, name=f"w1_raw{o}", tag=tag, align_bytes=ALIGN)
             rows = w1[o * K_PASS : (o + 1) * K_PASS, :]
             nc.sync.dma_start(w1_raw[o][:], rows.rearrange("(p j) c -> p j c", j=PACK))
 
         def move_scales(o, tag):
-            x_scale[o] = keep.tile([P, S], U8, name=f"x_scale{o}", tag=tag, align_bytes=64)
+            x_scale[o] = keep.tile([P, S], U8, name=f"x_scale{o}", tag=tag, align_bytes=ALIGN)
             rows = [(FIRST_ROW + o * PASS_ROWS + q * SCALE_ROWS, QUADRANT * q + X_ROW[o]) for q in range(QUADRANTS)]
             in_place = rows[-1][0] == rows[-1][1]
             zeroed = FIRST_ROW if in_place else P
@@ -97,35 +98,35 @@ def tile_picked_sub_mlp_silu_sub_p_kernel(
 
         x_codes = {}
         w1_bf = {
-            (o, u): keep.tile([P, PAIR * P * PACK], BF16, name=f"w1_bf{o}{u}", tag=f"bf{o}{u}", align_bytes=64)
+            (o, u): keep.tile([P, PAIR * P * PACK], BF16, name=f"w1_bf{o}{u}", tag=f"bf{o}{u}", align_bytes=ALIGN)
             for o in range(PASSES)
             for u in range(PAIR)
         }
         w1_codes = {}
-        scale_tiles = [keep.tile([P, PAIR * P], U8, name=f"w1_scales{i}", align_bytes=64) for i in range(3)]
+        scale_tiles = [keep.tile([P, PAIR * P], U8, name=f"w1_scales{i}", align_bytes=ALIGN) for i in range(3)]
         w1_scales = {}
         for v in range(PAIR):
             w1_scales[0, v] = scale_tiles[0][:, v * P : (v + 1) * P]
             w1_scales[0, PAIR + v] = scale_tiles[1 + v][:, :P]
             for u in range(PAIR):
                 w1_scales[1, PAIR * u + v] = scale_tiles[1 + u][SCALE_ROWS:, v * P : (v + 1) * P]
-        w2_codes = keep.tile([P, N], U32, name="w2_codes", align_bytes=64)
-        w2_scales = keep.tile([P, N], U8, name="w2_scales", align_bytes=64)
+        w2_codes = keep.tile([P, N], U32, name="w2_codes", align_bytes=ALIGN)
+        w2_scales = keep.tile([P, N], U8, name="w2_scales", align_bytes=ALIGN)
         pre = {c: psum.tile([P, PACK, CHUNK], F32, name=f"pre{c}", tag=f"bank{c}") for c in range(1, CHUNKS)}
         head = {
             t0: psum.tile([P, t1 - t0, CHUNK], F32, name=f"head{t0}", tag=f"bank{b}")
             for b, (t0, t1) in zip((0, CHUNKS, CHUNKS + 1), HEAD)
         }
-        h_planes = keep.tile([P, PACK, CHUNK], BF16, name="h_planes", align_bytes=64)
+        h_planes = keep.tile([P, PACK, CHUNK], BF16, name="h_planes", align_bytes=ALIGN)
         widths = [j1 - j0 for j0, j1 in GROUPS]
-        h_bf = [keep.tile([P, n * PACK], BF16, name=f"h_bf{g}", align_bytes=64) for g, n in enumerate(widths)]
+        h_bf = [keep.tile([P, n * PACK], BF16, name=f"h_bf{g}", align_bytes=ALIGN) for g, n in enumerate(widths)]
         h_codes = {}
-        h_scales = [keep.tile([P, n], U8, name=f"h_scales{g}", align_bytes=64) for g, n in enumerate(widths)]
+        h_scales = [keep.tile([P, n], U8, name=f"h_scales{g}", align_bytes=ALIGN) for g, n in enumerate(widths)]
         y_sb = keep.tile([P, S], F32, name="y_sb")
         y_ps = {}
 
         def gather_words(o):
-            codes = keep.tile([P, S], U32, name=f"x_codes{o}", align_bytes=64)
+            codes = keep.tile([P, S], U32, name=f"x_codes{o}", align_bytes=ALIGN)
             j = 0
             for n in GATHERS[o]:
                 entries = offs_sb[:, j // STRIPE : (j + n) // STRIPE]
@@ -146,7 +147,7 @@ def tile_picked_sub_mlp_silu_sub_p_kernel(
             nc.scalar.copy(dst[1][:, extra:], src[:, 1, extra:])
 
         def quantize_w1(o, u, tag):
-            codes = keep.tile([P, PAIR * P], U32, name=f"w1_codes{o}{u}", tag=tag, align_bytes=64)
+            codes = keep.tile([P, PAIR * P], U32, name=f"w1_codes{o}{u}", tag=tag, align_bytes=ALIGN)
             for v in range(PAIR):
                 w1_codes[o, PAIR * u + v] = codes[:, v * P : (v + 1) * P]
             if (o, u) != (0, 1):
@@ -171,7 +172,7 @@ def tile_picked_sub_mlp_silu_sub_p_kernel(
                 )
 
         def quantize_h(g, tag):
-            h_codes[g] = keep.tile([P, widths[g]], U32, name=f"h_codes{g}", tag=tag, align_bytes=64)
+            h_codes[g] = keep.tile([P, widths[g]], U32, name=f"h_codes{g}", tag=tag, align_bytes=ALIGN)
             nc.vector.quantize_mx(h_codes[g][:].bitcast(FP8X4), h_scales[g][:], h_bf[g][:])
 
         def layer2(g):
@@ -211,18 +212,18 @@ def tile_picked_sub_mlp_silu_sub_p_kernel(
             quantize_w1(1, u, f"codes1{u}")
             for c in range(CHUNKS):
                 layer1(0, c, [PAIR + u])
-        w2_raw = keep.tile([P, PACK, N], F32, name="w2_raw", tag="words0", align_bytes=64)
+        w2_raw = keep.tile([P, PACK, N], F32, name="w2_raw", tag="words0", align_bytes=ALIGN)
         for u in range(PAIR):
             nc.sync.dma_start(
                 w2_raw[:, PAIR * u : PAIR * (u + 1), :].rearrange("p v m -> p (v m)"),
                 w2.rearrange("(a u r v) m -> u a r (v m)", u=PAIR, r=2, v=PAIR)[u],
             )
         gather_words(1)
-        gate_sb = keep.tile([P, D, V], F32, name="gate_sb", tag="bf11", align_bytes=64)
+        gate_sb = keep.tile([P, D, V], F32, name="gate_sb", tag="bf11", align_bytes=ALIGN)
         nc.sync.dma_start(gate_sb[:], gate.rearrange("d m v -> m d v"))
         nc.sync.dma_start(pos_sb[0][:], pos1)
         nc.sync.dma_start(pos_sb[1][:], pos2)
-        w2_bf = keep.tile([P, N * PACK], BF16, name="w2_bf", tag="raw0", align_bytes=64)
+        w2_bf = keep.tile([P, N * PACK], BF16, name="w2_bf", tag="raw0", align_bytes=ALIGN)
         nc.vector.tensor_copy(
             w2_bf[:].rearrange("p (a m t) -> p a t m", m=RUN, t=PACK),
             w2_raw[:].rearrange("p t (a m) -> p a t m", m=RUN),
@@ -260,6 +261,6 @@ def tile_picked_sub_mlp_silu_sub_p_kernel(
         nc.vector.tensor_tensor(second[:, a0:a1], y_sb[:].indirect(entries), gate_sb[:, 1, a0:a1], MULT)
         nc.vector.tensor_tensor(second[:, b0:b1], fetched[:], gate_sb[:, 1, b0:b1], MULT)
         for i, (v0, v1) in enumerate(V_PIECES):
-            res = keep.tile([P, v1 - v0], F32, name=f"res{i}")
+            res = keep.tile([P, v1 - v0], F32, name=f"res{i}", align_bytes=ALIGN)
             nc.vector.tensor_add(res[:], first[:, v0:v1], second[:, v0:v1])
             nc.sync.dma_start(out[:, v0:v1], res[:])

@@ -35,7 +35,7 @@ BANKS = 8
 CHUNK = 128
 CHUNKS = S // CHUNK
 WIDEST = 256
-GATHERS = ((256, 256, 256), (128, 128, 256, 256))
+GATHERS = ((768,), (128, 128, 256, 256))
 VECTOR_EXTRA = (16, 0)
 GROUPS = ((0, 256), (256, 512), (512, 640), (640, 704), (704, 768))
 HEAD = ((0, 1), (1, 2), (2, 4))
@@ -85,17 +85,6 @@ def tile_picked_sub_mlp_silu_sub_p_kernel(
             if in_place:
                 nc.vector.tensor_copy(x_scale[o][zeroed:, :].bitcast(I32), scales_picked[zeroed:, :].bitcast(I32))
 
-        nc.sync.dma_start(scales_all[FIRST_ROW:, :], x_scales.rearrange("o q c -> (o q) c").bitcast(I32))
-        nc.sync.dma_start(offs_sb[:], offs)
-        nc.vector.memset(scales_all[:FIRST_ROW, :], 0)
-        load_w1(0, "raw0")
-        nc.vector.memset(zero[:], 0.0)
-        nc.scalar.activation(silu_zero[:], zero[:], SILU)
-        load_words(0, "words0")
-        nc.vector.tensor_copy(scales_picked[:], scales_all[:].bitcast(U8).indirect(offs_sb[:]))
-        move_scales(0, "x_scale0")
-        load_w1(1, "scales")
-
         x_codes = {}
         w1_bf = {
             (o, u): keep.tile([P, PAIR * P * PACK], BF16, name=f"w1_bf{o}{u}", tag=f"bf{o}{u}", align_bytes=ALIGN)
@@ -103,13 +92,7 @@ def tile_picked_sub_mlp_silu_sub_p_kernel(
             for u in range(PAIR)
         }
         w1_codes = {}
-        scale_tiles = [keep.tile([P, PAIR * P], U8, name=f"w1_scales{i}", align_bytes=ALIGN) for i in range(3)]
         w1_scales = {}
-        for v in range(PAIR):
-            w1_scales[0, v] = scale_tiles[0][:, v * P : (v + 1) * P]
-            w1_scales[0, PAIR + v] = scale_tiles[1 + v][:, :P]
-            for u in range(PAIR):
-                w1_scales[1, PAIR * u + v] = scale_tiles[1 + u][SCALE_ROWS:, v * P : (v + 1) * P]
         w2_codes = keep.tile([P, N], U32, name="w2_codes", align_bytes=ALIGN)
         w2_scales = keep.tile([P, N], U8, name="w2_scales", align_bytes=ALIGN)
         pre = {c: psum.tile([P, PACK, CHUNK], F32, name=f"pre{c}", tag=f"bank{c}") for c in range(1, CHUNKS)}
@@ -146,17 +129,13 @@ def tile_picked_sub_mlp_silu_sub_p_kernel(
                 nc.vector.tensor_copy(dst[1][:, :extra], src[:, 1, :extra])
             nc.scalar.copy(dst[1][:, extra:], src[:, 1, extra:])
 
-        def quantize_w1(o, u, tag):
-            codes = keep.tile([P, PAIR * P], U32, name=f"w1_codes{o}{u}", tag=tag, align_bytes=ALIGN)
+        def quantize_w1(o, u):
+            codes = keep.tile([P, PAIR * P], U32, name=f"w1_codes{o}{u}", align_bytes=ALIGN)
+            scales = keep.tile([P, PAIR * P], U8, name=f"w1_scales{o}{u}", align_bytes=ALIGN)
+            nc.vector.quantize_mx(codes[:].bitcast(FP8X4), scales[:], w1_bf[o, u][:])
             for v in range(PAIR):
                 w1_codes[o, PAIR * u + v] = codes[:, v * P : (v + 1) * P]
-            if (o, u) != (0, 1):
-                scales = scale_tiles[o + u][SCALE_ROWS * o :, :]
-                nc.vector.quantize_mx(codes[:].bitcast(FP8X4), scales, w1_bf[o, u][:])
-                return
-            for v in range(PAIR):
-                values = w1_bf[o, u][:, v * P * PACK : (v + 1) * P * PACK]
-                nc.vector.quantize_mx(w1_codes[o, PAIR + v].bitcast(FP8X4), w1_scales[o, PAIR + v], values)
+                w1_scales[o, PAIR * u + v] = scales[:, v * P : (v + 1) * P]
 
         def layer1(o, c, planes):
             for t in planes:
@@ -199,20 +178,29 @@ def tile_picked_sub_mlp_silu_sub_p_kernel(
             else:
                 nc.scalar.copy(y_sb[:, b0:b1], y_ps[b][:])
 
-        cast_w1(0)
-        load_words(1, "raw0")
-        quantize_w1(0, 0, "codes00")
-        quantize_w1(0, 1, "codes01")
-        move_scales(1, "bf00")
+        nc.sync.dma_start(scales_all[FIRST_ROW:, :], x_scales.rearrange("o q c -> (o q) c").bitcast(I32))
+        nc.sync.dma_start(offs_sb[:], offs)
+        nc.vector.memset(scales_all[:FIRST_ROW, :], 0)
+        load_words(0, "words")
+        load_w1(0, "raw0")
+        nc.vector.memset(zero[:], 0.0)
+        nc.scalar.activation(silu_zero[:], zero[:], SILU)
+        nc.vector.tensor_copy(scales_picked[:], scales_all[:].bitcast(U8).indirect(offs_sb[:]))
+        move_scales(0, "x_scale0")
+        load_w1(1, "scales")
         gather_words(0)
-        for c in range(CHUNKS):
-            layer1(0, c, range(PAIR))
+        load_words(1, "words")
+        cast_w1(0)
+        quantize_w1(0, 0)
+        move_scales(1, "bf00")
+        quantize_w1(0, 1)
+        for u in range(PAIR):
+            for c in range(CHUNKS):
+                layer1(0, c, range(PAIR * u, PAIR * (u + 1)))
         cast_w1(1)
         for u in range(PAIR):
-            quantize_w1(1, u, f"codes1{u}")
-            for c in range(CHUNKS):
-                layer1(0, c, [PAIR + u])
-        w2_raw = keep.tile([P, PACK, N], F32, name="w2_raw", tag="words0", align_bytes=ALIGN)
+            quantize_w1(1, u)
+        w2_raw = keep.tile([P, PACK, N], F32, name="w2_raw", tag="bf01", align_bytes=ALIGN)
         for u in range(PAIR):
             nc.sync.dma_start(
                 w2_raw[:, PAIR * u : PAIR * (u + 1), :].rearrange("p v m -> p (v m)"),
@@ -223,7 +211,7 @@ def tile_picked_sub_mlp_silu_sub_p_kernel(
         nc.sync.dma_start(gate_sb[:], gate.rearrange("d m v -> m d v"))
         nc.sync.dma_start(pos_sb[0][:], pos1)
         nc.sync.dma_start(pos_sb[1][:], pos2)
-        w2_bf = keep.tile([P, N * PACK], BF16, name="w2_bf", tag="raw0", align_bytes=ALIGN)
+        w2_bf = keep.tile([P, N * PACK], BF16, name="w2_bf", tag="words", align_bytes=ALIGN)
         nc.vector.tensor_copy(
             w2_bf[:].rearrange("p (a m t) -> p a t m", m=RUN, t=PACK),
             w2_raw[:].rearrange("p t (a m) -> p a t m", m=RUN),

@@ -14,7 +14,6 @@ U8 = mybir.dt.uint8
 FP8X4 = mybir.dt.float8_e4m3fn_x4
 MULT = mybir.AluOpType.mult
 SILU = mybir.ActivationFunctionType.Silu
-IDENTITY = mybir.ActivationFunctionType.Identity
 COPY = mybir.ActivationFunctionType.Copy
 
 P = 128
@@ -59,8 +58,6 @@ def tile_picked_sub_mlp_silu_sub_p_kernel(
         x_scale = {}
         scales_all = keep.tile([P, T // PACK], I32, name="scales_all", tag="scales", align_bytes=ALIGN)
         w1_raw = {}
-        zero = keep.tile([P, 1], F32, name="zero")
-        silu_zero = keep.tile([P, 1], F32, name="silu_zero")
 
         def load_words(o, tag):
             words_all[o] = keep.tile([P, T], I32, name=f"words_all{o}", tag=tag, align_bytes=ALIGN)
@@ -173,18 +170,13 @@ def tile_picked_sub_mlp_silu_sub_p_kernel(
                 )
             if j1 < b1:
                 return
-            if b == 0:
-                nc.scalar.activation(y_sb[:, b0:b1], y_ps[b][:], IDENTITY, bias=silu_zero[:])
-            else:
-                nc.scalar.copy(y_sb[:, b0:b1], y_ps[b][:])
+            nc.scalar.copy(y_sb[:, b0:b1], y_ps[b][:])
 
         nc.sync.dma_start(scales_all[FIRST_ROW:, :], x_scales.rearrange("o q c -> (o q) c").bitcast(I32))
         nc.sync.dma_start(offs_sb[:], offs)
         nc.vector.memset(scales_all[:FIRST_ROW, :], 0)
         load_words(0, "words")
         load_w1(0, "raw0")
-        nc.vector.memset(zero[:], 0.0)
-        nc.scalar.activation(silu_zero[:], zero[:], SILU)
         nc.vector.tensor_copy(scales_picked[:], scales_all[:].bitcast(U8).indirect(offs_sb[:]))
         move_scales(0, "x_scale0")
         load_w1(1, "scales")

@@ -34,7 +34,7 @@ BANKS = 8
 CHUNK = 128
 CHUNKS = S // CHUNK
 WIDEST = 256
-GATHERS = ((768,), (128, 128, 256, 256))
+GATHERS = ((768,), (128, 128, 128, 128, 256))
 VECTOR_EXTRA = (16, 0)
 GROUPS = ((0, 256), (256, 512), (512, 640), (640, 704), (704, 768))
 HEAD = ((0, 1), (1, 2), (2, 4))

@@ -35,7 +35,7 @@ CHUNK = 128
 CHUNKS = S // CHUNK
 WIDEST = 256
 GATHERS = ((768,), (128, 128, 128, 128, 256))
-VECTOR_EXTRA = (16, 0)
+VECTOR_EXTRA = (16, 16)
 GROUPS = ((0, 256), (256, 512), (512, 640), (640, 704), (704, 768))
 HEAD = ((0, 1), (1, 2), (2, 4))
 Y_BANKS = ((0, 1), (2, 3), (4,))

@@ -239,8 +239,10 @@ def tile_picked_sub_mlp_silu_sub_p_kernel(
         nc.vector.tensor_tensor(first[:], y_sb[:].indirect(pos_sb[0][:]), gate_sb[:, 0, :], MULT)
         entries = pos_sb[1][:, a0 // STRIPE : a1 // STRIPE]
         nc.vector.tensor_tensor(second[:, a0:a1], y_sb[:].indirect(entries), gate_sb[:, 1, a0:a1], MULT)
-        nc.vector.tensor_tensor(second[:, b0:b1], fetched[:], gate_sb[:, 1, b0:b1], MULT)
         for i, (v0, v1) in enumerate(V_PIECES):
+            if v1 < V:
+                n0, n1 = V_PIECES[i + 1]
+                nc.vector.tensor_tensor(second[:, n0:n1], fetched[:, n0 - b0 : n1 - b0], gate_sb[:, 1, n0:n1], MULT)
             res = keep.tile([P, v1 - v0], F32, name=f"res{i}", align_bytes=ALIGN)
             nc.vector.tensor_add(res[:], first[:, v0:v1], second[:, v0:v1])
             nc.sync.dma_start(out[:, v0:v1], res[:])

from contextlib import ExitStack

import concourse.mybir as mybir

K, T, D, S, V, H, N = 1024, 2048, 2, 768, 384, 512, 128
FLOPS = 2 * K * H * S + 2 * H * N * S

F32 = mybir.dt.float32
BF16 = mybir.dt.bfloat16
I32 = mybir.dt.int32
U32 = mybir.dt.uint32
U16 = mybir.dt.uint16
U8 = mybir.dt.uint8
FP8X4 = mybir.dt.float8_e4m3fn_x4
MULT = mybir.AluOpType.mult
SILU = mybir.ActivationFunctionType.Silu
COPY = mybir.ActivationFunctionType.Copy

P = 128
ALIGN = 256
PACK = 4
PAIR = 2
K_PASS = P * PACK
PASSES = K // K_PASS
QUADRANT = 32
QUADRANTS = P // QUADRANT
SCALE_ROWS = 4
PASS_ROWS = QUADRANTS * SCALE_ROWS
FIRST_ROW = P - PASSES * PASS_ROWS
X_ROW = (12, 4)
STRIPE = 16
RUN = 4
BANKS = 8
CHUNK = 128
CHUNKS = S // CHUNK
WIDEST = 256
GATHERS = ((768,), (128, 128, 128, 128, 256))
VECTOR_EXTRA = (16, 16)
GROUPS = ((0, 256), (256, 512), (512, 640), (640, 704), (704, 768))
HEAD = ((0, 1), (1, 2), (2, 4))
Y_BANKS = ((0, 1), (2, 3), (4,))
OWN = 128
V_PIECES = ((0, 128), (128, 256), (256, 384))


def tile_picked_sub_mlp_silu_sub_p_kernel(
    tc, x_words, x_scales, w1, w2, gate, offs, pos1, pos2, out
):
    nc = tc.nc
    with ExitStack() as ctx:
        keep = ctx.enter_context(tc.tile_pool(name="keep", bufs=1))
        psum = ctx.enter_context(tc.psum_pool(name="psum", bufs=1))

        offs_sb = keep.tile([P, S // STRIPE], U16, name="offs_sb")
        pos_sb = [keep.tile([P, V // STRIPE], U16, name=f"pos_sb{d}") for d in range(D)]
        words_all = {}
        scales_picked = keep.tile([P, S], U8, name="scales_picked", align_bytes=ALIGN)
        x_scale = {}
        scales_all = keep.tile([P, T // PACK], I32, name="scales_all", tag="scales", align_bytes=ALIGN)
        w1_raw = {}

        def load_words(o, tag):
            words_all[o] = keep.tile([P, T], I32, name=f"words_all{o}", tag=tag, align_bytes=ALIGN)
            nc.sync.dma_start(words_all[o][:], x_words[o].rearrange("p n t -> p (n t)").bitcast(I32))

        def load_w1(o, tag):
            w1_raw[o] = keep.tile([P, PACK, H], F32, name=f"w1_raw{o}", tag=tag, align_bytes=ALIGN)
            rows = w1[o * K_PASS : (o + 1) * K_PASS, :]
            nc.sync.dma_start(w1_raw[o][:], rows.rearrange("(p j) c -> p j c", j=PACK))

        def move_scales(o, tag):
            x_scale[o] = keep.tile([P, S], U8, name=f"x_scale{o}", tag=tag, align_bytes=ALIGN)
            rows = [(FIRST_ROW + o * PASS_ROWS + q * SCALE_ROWS, QUADRANT * q + X_ROW[o]) for q in range(QUADRANTS)]
            in_place = rows[-1][0] == rows[-1][1]
            zeroed = FIRST_ROW if in_place else P
            nc.vector.memset(x_scale[o][:zeroed, :].bitcast(I32), 0)
            for src, dst in rows[: zeroed // QUADRANT]:
                nc.sync.dma_start(
                    x_scale[o][dst : dst + SCALE_ROWS, :].bitcast(I32),
                    scales_picked[src : src + SCALE_ROWS, :].bitcast(I32),
                )
            if in_place:
                nc.vector.tensor_copy(x_scale[o][zeroed:, :].bitcast(I32), scales_picked[zeroed:, :].bitcast(I32))

        x_codes = {}
        w1_bf = {
            (o, u): keep.tile([P, PAIR * P * PACK], BF16, name=f"w1_bf{o}{u}", tag=f"bf{o}{u}", align_bytes=ALIGN)
            for o in range(PASSES)
            for u in range(PAIR)
        }
        w1_codes = {}
        w1_scales = {}
        w2_codes = keep.tile([P, N], U32, name="w2_codes", align_bytes=ALIGN)
        w2_scales = keep.tile([P, N], U8, name="w2_scales", align_bytes=ALIGN)
        pre = {c: psum.tile([P, PACK, CHUNK], F32, name=f"pre{c}", tag=f"bank{c}") for c in range(1, CHUNKS)}
        head = {
            t0: psum.tile([P, t1 - t0, CHUNK], F32, name=f"head{t0}", tag=f"bank{b}")
            for b, (t0, t1) in zip((0, CHUNKS, CHUNKS + 1), HEAD)
        }
        h_planes = keep.tile([P, PACK, CHUNK], BF16, name="h_planes", align_bytes=ALIGN)
        widths = [j1 - j0 for j0, j1 in GROUPS]
        h_bf = [keep.tile([P, n * PACK], BF16, name=f"h_bf{g}", align_bytes=ALIGN) for g, n in enumerate(widths)]
        h_codes = {}
        h_scales = [keep.tile([P, n], U8, name=f"h_scales{g}", align_bytes=ALIGN) for g, n in enumerate(widths)]
        y_sb = keep.tile([P, S], F32, name="y_sb")
        y_ps = {}

        def gather_words(o):
            codes = keep.tile([P, S], U32, name=f"x_codes{o}", align_bytes=ALIGN)
            j = 0
            for n in GATHERS[o]:
                entries = offs_sb[:, j // STRIPE : (j + n) // STRIPE]
                nc.vector.tensor_copy(codes[:, j : j + n], words_all[o][:].bitcast(U32).indirect(entries))
                j = j + n
            for c in range(CHUNKS):
                x_codes[o, c] = codes[:, c * CHUNK : (c + 1) * CHUNK]

        def cast_w1(o):
            src = w1_raw[o][:].rearrange("p j (a u r v) -> p u a j r v", u=PAIR, r=2, v=PAIR)
            dst = [
                w1_bf[o, u][:].rearrange("p (v a r j) -> p a j r v", v=PAIR, r=2, j=PACK) for u in range(PAIR)
            ]
            nc.vector.tensor_copy(dst[0], src[:, 0])
            extra = VECTOR_EXTRA[o]
            if extra:
                nc.vector.tensor_copy(dst[1][:, :extra], src[:, 1, :extra])
            nc.scalar.copy(dst[1][:, extra:], src[:, 1, extra:])

        def quantize_w1(o, u):
            codes = keep.tile([P, PAIR * P], U32, name=f"w1_codes{o}{u}", align_bytes=ALIGN)
            scales = keep.tile([P, PAIR * P], U8, name=f"w1_scales{o}{u}", align_bytes=ALIGN)
            nc.vector.quantize_mx(codes[:].bitcast(FP8X4), scales[:], w1_bf[o, u][:])
            for v in range(PAIR):
                w1_codes[o, PAIR * u + v] = codes[:, v * P : (v + 1) * P]
                w1_scales[o, PAIR * u + v] = scales[:, v * P : (v + 1) * P]

        def layer1(o, c, planes):
            for t in planes:
                t0, t1 = (0, PACK) if c else [span for span in HEAD if t < span[1]][0]
                nc.tensor.matmul_mx(
                    (pre[c] if c else head[t0])[:, t - t0, :],
                    lhsT=w1_codes[o, t].bitcast(FP8X4),
                    lhsT_scale=w1_scales[o, t],
                    rhs=x_codes[o, c].bitcast(FP8X4),
                    rhs_scale=x_scale[o][X_ROW[o] :, c * CHUNK : (c + 1) * CHUNK],
                    start=(o == 0 and t == t0),
                    stop=(o == PASSES - 1 and t == t1 - 1),
                )

        def quantize_h(g, tag):
            h_codes[g] = keep.tile([P, widths[g]], U32, name=f"h_codes{g}", tag=tag, align_bytes=ALIGN)
            nc.vector.quantize_mx(h_codes[g][:].bitcast(FP8X4), h_scales[g][:], h_bf[g][:])

        def layer2(g):
            j0, j1 = GROUPS[g]
            b = [g in members for members in Y_BANKS].index(True)
            b0, b1 = GROUPS[Y_BANKS[b][0]][0], GROUPS[Y_BANKS[b][-1]][1]
            if b not in y_ps:
                y_ps[b] = psum.tile([P, b1 - b0], F32, name=f"y_ps{b}", tag=f"bank{(CHUNKS + b) % BANKS}")
            for j in range(j0, j1, WIDEST):
                n = min(WIDEST, j1 - j)
                nc.tensor.matmul_mx(
                    y_ps[b][:, j - b0 : j - b0 + n],
                    lhsT=w2_codes[:].bitcast(FP8X4),
                    lhsT_scale=w2_scales[:],
                    rhs=h_codes[g][:, j - j0 : j - j0 + n].bitcast(FP8X4),
                    rhs_scale=h_scales[g][:, j - j0 : j - j0 + n],
                    start=True,
                    stop=True,
                )
            if j1 < b1:
                return
            nc.scalar.copy(y_sb[:, b0:b1], y_ps[b][:])

        nc.sync.dma_start(scales_all[FIRST_ROW:, :], x_scales.rearrange("o q c -> (o q) c").bitcast(I32))
        nc.sync.dma_start(offs_sb[:], offs)
        nc.vector.memset(scales_all[:FIRST_ROW, :], 0)
        load_words(0, "words")
        load_w1(0, "raw0")
        nc.vector.tensor_copy(scales_picked[:], scales_all[:].bitcast(U8).indirect(offs_sb[:]))
        move_scales(0, "x_scale0")
        load_w1(1, "scales")
        gather_words(0)
        load_words(1, "words")
        cast_w1(0)
        quantize_w1(0, 0)
        move_scales(1, "bf00")
        quantize_w1(0, 1)
        for u in range(PAIR):
            for c in range(CHUNKS):
                layer1(0, c, range(PAIR * u, PAIR * (u + 1)))
        cast_w1(1)
        for u in range(PAIR):
            quantize_w1(1, u)
        w2_raw = keep.tile([P, PACK, N], F32, name="w2_raw", tag="bf01", align_bytes=ALIGN)
        for u in range(PAIR):
            nc.sync.dma_start(
                w2_raw[:, PAIR * u : PAIR * (u + 1), :].rearrange("p v m -> p (v m)"),
                w2.rearrange("(a u r v) m -> u a r (v m)", u=PAIR, r=2, v=PAIR)[u],
            )
        gather_words(1)
        gate_sb = keep.tile([P, D, V], F32, name="gate_sb", tag="bf11", align_bytes=ALIGN)
        nc.sync.dma_start(gate_sb[:], gate.rearrange("d m v -> m d v"))
        nc.sync.dma_start(pos_sb[0][:], pos1)
        nc.sync.dma_start(pos_sb[1][:], pos2)
        w2_bf = keep.tile([P, N * PACK], BF16, name="w2_bf", tag="words", align_bytes=ALIGN)
        nc.vector.tensor_copy(
            w2_bf[:].rearrange("p (a m t) -> p a t m", m=RUN, t=PACK),
            w2_raw[:].rearrange("p t (a m) -> p a t m", m=RUN),
        )
        for c in range(CHUNKS):
            layer1(1, c, range(PACK))

        for t0, t1 in HEAD:
            nc.scalar.activation(h_planes[:, t0:t1, :], head[t0][:], SILU)
        nc.vector.tensor_copy(
            h_bf[0][:, : CHUNK * PACK].rearrange("p (a m t) -> p a t m", m=RUN, t=PACK),
            h_planes[:].rearrange("p t (a m) -> p a t m", m=RUN),
        )
        for g, (j0, j1) in enumerate(GROUPS):
            for j in range(max(j0, CHUNK), j1, CHUNK):
                n = min(CHUNK, j1 - j)
                h_out = h_bf[g][:, (j - j0) * PACK : (j - j0 + n) * PACK]
                nc.scalar.activation(
                    h_out.rearrange("p (n t) -> p n t", t=PACK),
                    pre[j // CHUNK][:, :, j % CHUNK : j % CHUNK + n].rearrange("p t n -> p n t"),
                    SILU,
                )
        nc.vector.quantize_mx(w2_codes[:].bitcast(FP8X4), w2_scales[:], w2_bf[:])
        for g in range(len(GROUPS)):
            quantize_h(g, f"h_codes{g}")
            layer2(g)

        a0, a1, b0, b1 = 0, OWN, OWN, V
        first = keep.tile([P, V], F32, name="first")
        second = keep.tile([P, V], F32, name="second")
        fetched = keep.tile([P, b1 - b0], F32, name="fetched")
        nc.scalar.activation(fetched[:], y_sb[:].indirect(pos_sb[1][:, b0 // STRIPE : b1 // STRIPE]), COPY)
        nc.vector.tensor_tensor(first[:], y_sb[:].indirect(pos_sb[0][:]), gate_sb[:, 0, :], MULT)
        entries = pos_sb[1][:, a0 // STRIPE : a1 // STRIPE]
        nc.vector.tensor_tensor(second[:, a0:a1], y_sb[:].indirect(entries), gate_sb[:, 1, a0:a1], MULT)
        for i, (v0, v1) in enumerate(V_PIECES):
            if v1 < V:
                n0, n1 = V_PIECES[i + 1]
                nc.vector.tensor_tensor(second[:, n0:n1], fetched[:, n0 - b0 : n1 - b0], gate_sb[:, 1, n0:n1], MULT)
            res = keep.tile([P, v1 - v0], F32, name=f"res{i}", align_bytes=ALIGN)
            nc.vector.tensor_add(res[:], first[:, v0:v1], second[:, v0:v1])
            nc.sync.dma_start(out[:, v0:v1], res[:])
